import numpy as np
import ml_dtypes


def mxq(x, axis, fmt="e4m3"):
    dtype, down = {"e4m3": (ml_dtypes.float8_e4m3fn, 7), "e5m2": (ml_dtypes.float8_e5m2, 14)}[fmt]
    v = np.moveaxis(np.asarray(x, np.float32).astype(ml_dtypes.bfloat16).astype(np.float64), axis, -1)
    blocks = v.reshape(v.shape[:-1] + (-1, 32))
    amax = np.abs(blocks).max(-1, keepdims=True)
    byte = np.maximum(np.where(amax > 0, np.frexp(amax)[1] - 1 + 127, 0) - down, 1)
    scale = np.exp2(byte - 127.0)
    codes = (blocks / scale).astype(np.float32).astype(dtype).astype(np.float64)
    return np.moveaxis((codes * scale).reshape(v.shape), -1, axis)


WIDE = False


def mx_kscale(k):
    if not WIDE:
        return np.ones(k)
    levels = np.array([10, -10, 5, -5, 0])
    if k % 512:
        return np.exp2(np.random.permutation(np.resize(levels, k // 32))).repeat(32)
    a = np.empty((k // 512, 16))
    for p in range(k // 512):
        a[p, :8] = np.random.permutation(np.resize(levels, 8))
        for g in range(8):
            far = levels[np.abs(levels - a[p, g]) >= 10]
            a[p, g + 8] = far[np.random.randint(len(far))]
    return np.exp2(a.ravel()).repeat(32)


def f64(x):
    return np.asarray(x).astype(np.float64)


def striped(idx):
    return np.tile(idx.reshape(-1, 16).T, (8, 1)).astype(np.uint16)


def unstriped(offs):
    return offs[:16].T.reshape(-1).astype(np.int64)


def gelu(v):
    return 0.5 * v * (1.0 + np.tanh(np.sqrt(2.0 / np.pi) * (v + 0.044715 * v**3)))


K, T, S, H, N = 1024, 2048, 1024, 512, 128


def setup_inputs():
    n = np.random.standard_normal
    s = mx_kscale(K)[:, None]
    u = mx_kscale(H)
    return {
        "xT": (n((K, T)) * s).astype(np.float32),
        "w1": (n((K, H)) / np.sqrt(K) / s * u).astype(np.float32),
        "w2": (n((H, N)) / np.sqrt(H) / u[:, None]).astype(np.float32),
        "pos": (0.5 * n((H, S)) * u[:, None]).astype(np.float32),
        "offs": striped(np.random.permutation(T)[(T * np.random.uniform(0, 1, S) ** 4).astype(np.int64)]),
    }


def reference(xT, w1, w2, pos, offs):
    xq = mxq(f64(xT)[:, unstriped(offs)], 0, "e4m3")
    h = gelu((mxq(f64(w1), 0, "e4m3").T @ xq) + f64(pos))
    return mxq(f64(w2), 0, "e4m3").T @ mxq(h, 0, "e4m3")

@@ -1,0 +1,215 @@
+from contextlib import ExitStack
+
+import concourse.mybir as mybir
+
+K, T, S, H, N = 1024, 2048, 1024, 512, 128
+FLOPS = 2 * S * (K * H + H * N)
+
+F32 = mybir.dt.float32
+BF16 = mybir.dt.bfloat16
+I32 = mybir.dt.int32
+U32 = mybir.dt.uint32
+U16 = mybir.dt.uint16
+U8 = mybir.dt.uint8
+FP8X4 = mybir.dt.float8_e4m3fn_x4
+GELU = mybir.ActivationFunctionType.Gelu_apprx_tanh
+ADD = mybir.AluOpType.add
+
+P = 128
+PACK = 4
+K_PASS = P * PACK
+PASSES = K // K_PASS
+HALF = 512
+X_CHUNKS = ((512, 512, 512, 512), (512, 512, 512, 256, 256))
+POS_CHUNKS = (256, 256, 512)
+H_CHUNKS = (128, 128, 256, 256, 128, 128)
+
+
+def starts(widths):
+    return [sum(widths[:i]) for i in range(len(widths))]
+
+
+def weave_views(dst, src):
+    return (
+        dst.rearrange("p (c i t) -> p c t i", i=4, t=PACK),
+        src.rearrange("p t (c i) -> p c t i", i=4),
+    )
+
+
+def tile_picked_embpos_gelu_e_kernel(tc, xT, w1, w2, pos, offs, out):
+    nc = tc.nc
+    with ExitStack() as ctx:
+        lists = ctx.enter_context(tc.tile_pool(name="lists", bufs=1))
+        sb = ctx.enter_context(tc.tile_pool(name="sb", bufs=1))
+        psum = ctx.enter_context(tc.psum_pool(name="psum", bufs=1))
+
+        offsets = lists.tile([P, S // 16], U16, name="offsets")
+        x_scales = sb.tile([P, T], U8, name="x_scales", align_bytes=64)
+        nc.vector.memset(x_scales[:].bitcast(I32), 0)
+        x_words = [sb.tile([P, T], U32, name="x_words%d" % g, align_bytes=64) for g in range(PASSES)]
+
+        x_raw = {}
+        for g in range(PASSES):
+            rows = xT[g * K_PASS : (g + 1) * K_PASS, :].rearrange("(p j) c -> p j c", j=PACK)
+            for c0, width in zip(starts(X_CHUNKS[g]), X_CHUNKS[g]):
+                x_raw[g, c0] = sb.tile([P, PACK, width], F32, name="x_raw%d_%d" % (g, c0), align_bytes=64)
+                nc.sync.dma_start(out=x_raw[g, c0][:], in_=rows[:, :, c0 : c0 + width])
+            if g == 0:
+                nc.sync.dma_start(offsets[:], offs)
+        w1_raw = {}
+        for g in range(PASSES):
+            rows = w1[g * K_PASS : (g + 1) * K_PASS, :].rearrange("(p j) c -> p j c", j=PACK)
+            for a in range(2):
+                w1_raw[g, a] = sb.tile([P, PACK, H // 2], F32, name="w1_raw%d_%d" % (g, a), align_bytes=64)
+                nc.sync.dma_start(out=w1_raw[g, a][:], in_=rows[:, :, a * (H // 2) : (a + 1) * (H // 2)])
+        pos_rows = pos.rearrange("(p t) s -> p t s", t=PACK)
+        pos_sb = {}
+        w2_raw = sb.tile([P, PACK, N], F32, name="w2_raw", align_bytes=64)
+        for s0, width in zip(starts(POS_CHUNKS), POS_CHUNKS):
+            pos_sb[s0] = sb.tile([P, PACK, width], F32, name="pos%d" % s0, align_bytes=64)
+            nc.sync.dma_start(out=pos_sb[s0][:], in_=pos_rows[:, :, s0 : s0 + width])
+            if s0 == 0:
+                nc.sync.dma_start(out=w2_raw[:], in_=w2.rearrange("(p j) n -> p j n", j=PACK))
+
+        def quantise_x(g, c0, width):
+            half = width // 2
+            parts = []
+            for e in range(2):
+                woven = sb.tile([P, half * PACK], BF16, name="x_bf%d_%d_%d" % (g, c0, e), align_bytes=64)
+                dst, src = weave_views(woven[:], x_raw[g, c0][:, :, e * half : (e + 1) * half])
+                if e == 0:
+                    nc.vector.tensor_copy(out=dst, in_=src)
+                else:
+                    nc.scalar.copy(out=dst, in_=src)
+                parts.append(woven)
+            for e in range(2):
+                cols = slice(c0 + e * half, c0 + (e + 1) * half)
+                nc.vector.quantize_mx(
+                    out=x_words[g][:, cols].bitcast(FP8X4), scales=x_scales[PACK * g : P, cols], in_=parts[e][:]
+                )
+
+        picked_words = {}
+        picked_scales = {}
+
+        def gather_words(g, h):
+            picked_words[g, h] = sb.tile([P, HALF], U32, name="picked_words%d_%d" % (g, h), align_bytes=64)
+            nc.vector.tensor_copy(picked_words[g, h][:], x_words[g][:].indirect(offsets[:, 32 * h : 32 * (h + 1)]))
+
+        def gather_scales(h):
+            picked_scales[h] = sb.tile([P, HALF], U8, name="picked_scales%d" % h, align_bytes=64)
+            nc.vector.tensor_copy(picked_scales[h][:], x_scales[:].indirect(offsets[:, 32 * h : 32 * (h + 1)]))
+
+        w1_bf = [sb.tile([P, PACK, P, PACK], BF16, name="w1_bf%d" % g, align_bytes=64) for g in range(PASSES)]
+        w1_words = [sb.tile([P, H], U32, name="w1_words%d" % g, align_bytes=64) for g in range(PASSES)]
+        w1_scales = [sb.tile([P, H], U8, name="w1_scales%d" % g, align_bytes=64) for g in range(PASSES)]
+
+        def weave_w1(g, a, engine_copy):
+            dst = w1_bf[g][:, :, a * 64 : (a + 1) * 64, :].rearrange("p t m j -> p m t j")
+            src = w1_raw[g, a][:].rearrange("p j (m t) -> p m t j", t=PACK)
+            engine_copy(out=dst, in_=src)
+
+        def quantise_w1(g):
+            for t in range(PACK):
+                cols = slice(t * P, (t + 1) * P)
+                nc.vector.quantize_mx(
+                    out=w1_words[g][:, cols].bitcast(FP8X4),
+                    scales=w1_scales[g][:, cols],
+                    in_=w1_bf[g][:, t, :, :].rearrange("p m j -> p (m j)"),
+                )
+
+        acc = {}
+
+        def first_layer(g, h):
+            for t in range(PACK):
+                if g == 0:
+                    acc[h, t] = psum.tile([P, HALF], F32, name="acc%d_%d" % (h, t), tag="bank%d" % (PACK * h + t))
+                cols = slice(t * P, (t + 1) * P)
+                nc.tensor.matmul_mx(
+                    out=acc[h, t][:],
+                    lhsT=w1_words[g][:, cols].bitcast(FP8X4),
+                    lhsT_scale=w1_scales[g][:, cols],
+                    rhs=picked_words[g, h][:].bitcast(FP8X4),
+                    rhs_scale=picked_scales[h][PACK * g : P, :],
+                    start=(g == 0),
+                    stop=(g == PASSES - 1),
+                )
+
+        for c0, width in zip(starts(X_CHUNKS[0]), X_CHUNKS[0]):
+            quantise_x(0, c0, width)
+        later = list(zip(starts(X_CHUNKS[1]), X_CHUNKS[1]))
+        quantise_x(1, *later[0])
+        gather_words(0, 0)
+        quantise_x(1, *later[1])
+        gather_words(0, 1)
+        for c0, width in later[2:]:
+            quantise_x(1, c0, width)
+
+        gather_scales(0)
+        gather_words(1, 0)
+        weave_w1(0, 0, nc.scalar.copy)
+        weave_w1(0, 1, nc.scalar.copy)
+        gather_scales(1)
+        quantise_w1(0)
+        first_layer(0, 0)
+        gather_words(1, 1)
+        weave_w1(1, 0, nc.scalar.copy)
+        weave_w1(1, 1, nc.vector.tensor_copy)
+        quantise_w1(1)
+        first_layer(1, 0)
+        first_layer(0, 1)
+        first_layer(1, 1)
+
+        w2_bf = sb.tile([P, N * PACK], BF16, name="w2_bf", align_bytes=64)
+        w2_words = sb.tile([P, N], U32, name="w2_words", align_bytes=64)
+        w2_scales = sb.tile([P, N], U8, name="w2_scales", align_bytes=64)
+        dst, src = weave_views(w2_bf[:], w2_raw[:])
+        nc.scalar.copy(out=dst, in_=src)
+
+        h_bf = {}
+        h_words = {}
+        h_scales = {}
+
+        def hidden(s0, width):
+            h, off = divmod(s0, HALF)
+            p0 = max(q for q in pos_sb if q <= s0)
+            pre = sb.tile([P, PACK, width], F32, name="pre%d" % s0, align_bytes=64)
+            for t in range(PACK):
+                nc.vector.tensor_tensor(
+                    pre[:, t, :], acc[h, t][:, off : off + width], pos_sb[p0][:, t, s0 - p0 : s0 - p0 + width], ADD
+                )
+            h_bf[s0] = sb.tile([P, width * PACK], BF16, name="h_bf%d" % s0, align_bytes=64)
+            dst, src = weave_views(h_bf[s0][:], pre[:])
+            nc.scalar.activation(dst, src, GELU)
+
+        def quantise_h(s0, width):
+            h_words[s0] = sb.tile([P, width], U32, name="h_words%d" % s0, align_bytes=64)
+            h_scales[s0] = sb.tile([P, width], U8, name="h_scales%d" % s0, align_bytes=64)
+            nc.vector.quantize_mx(out=h_words[s0][:].bitcast(FP8X4), scales=h_scales[s0][:], in_=h_bf[s0][:])
+
+        def second_layer(i, s0, width):
+            res = psum.tile([P, width], F32, name="res%d" % s0, tag="bank%d" % (i % PACK))
+            nc.tensor.matmul_mx(
+                out=res[:],
+                lhsT=w2_words[:].bitcast(FP8X4),
+                lhsT_scale=w2_scales[:],
+                rhs=h_words[s0][:].bitcast(FP8X4),
+                rhs_scale=h_scales[s0][:],
+                start=True,
+                stop=True,
+            )
+            staged = sb.tile([P, width], F32, name="staged%d" % s0, align_bytes=64)
+            nc.scalar.copy(out=staged[:], in_=res[:])
+            nc.sync.dma_start(out=out[:, s0 : s0 + width], in_=staged[:])
+
+        chunks = list(zip(starts(H_CHUNKS), H_CHUNKS))
+        for i, (s0, width) in enumerate(chunks):
+            hidden(s0, width)
+            if i == 0:
+                nc.vector.quantize_mx(out=w2_words[:].bitcast(FP8X4), scales=w2_scales[:], in_=w2_bf[:])
+            if i >= 1:
+                quantise_h(*chunks[i - 1])
+            if i >= 3:
+                second_layer(i - 3, *chunks[i - 3])
+        quantise_h(*chunks[-1])
+        for i in range(len(chunks) - 3, len(chunks)):
+            second_layer(i, *chunks[i])

@@ -20,9 +20,12 @@ PACK = 4
 K_PASS = P * PACK
 PASSES = K // K_PASS
 HALF = 512
-X_CHUNKS = ((512, 512, 512, 512), (512, 512, 512, 256, 256))
-POS_CHUNKS = (256, 256, 512)
-H_CHUNKS = (128, 128, 256, 256, 128, 128)
+X_CHUNKS = ((1024, 512, 512), (512, 512, 512, 256, 256))
+UNIT = 512
+POS_CHUNKS = (512, 512)
+PICKS = (512, 256, 256)
+H_CHUNKS = (256, 256, 256, 128, 128)
+OUT_CHUNKS = (512, 256, 128, 128)
 
 
 def starts(widths):
@@ -46,6 +49,9 @@ def tile_picked_embpos_gelu_e_kernel(tc, xT, w1, w2, pos, offs, out):
         offsets = lists.tile([P, S // 16], U16, name="offsets")
         x_scales = sb.tile([P, T], U8, name="x_scales", align_bytes=64)
         nc.vector.memset(x_scales[:].bitcast(I32), 0)
+        warm = sb.tile([P, 2], F32, name="warm")
+        nc.vector.memset(warm[:, 0:1], 0.0)
+        nc.scalar.activation(warm[:, 1:2], warm[:, 0:1], GELU)
         x_words = [sb.tile([P, T], U32, name="x_words%d" % g, align_bytes=64) for g in range(PASSES)]
 
         x_raw = {}
@@ -60,7 +66,7 @@ def tile_picked_embpos_gelu_e_kernel(tc, xT, w1, w2, pos, offs, out):
         for g in range(PASSES):
             rows = w1[g * K_PASS : (g + 1) * K_PASS, :].rearrange("(p j) c -> p j c", j=PACK)
             for a in range(2):
-                w1_raw[g, a] = sb.tile([P, PACK, H // 2], F32, name="w1_raw%d_%d" % (g, a), align_bytes=64)
+                w1_raw[g, a] = sb.tile([P, PACK, H // 2], F32, name="w1_raw%d_%d" % (g, a), tag="w1_raw%d_%d" % (g, a), align_bytes=64)
                 nc.sync.dma_start(out=w1_raw[g, a][:], in_=rows[:, :, a * (H // 2) : (a + 1) * (H // 2)])
         pos_rows = pos.rearrange("(p t) s -> p t s", t=PACK)
         pos_sb = {}
@@ -72,92 +78,111 @@ def tile_picked_embpos_gelu_e_kernel(tc, xT, w1, w2, pos, offs, out):
                 nc.sync.dma_start(out=w2_raw[:], in_=w2.rearrange("(p j) n -> p j n", j=PACK))
 
         def quantise_x(g, c0, width):
-            half = width // 2
-            parts = []
-            for e in range(2):
-                woven = sb.tile([P, half * PACK], BF16, name="x_bf%d_%d_%d" % (g, c0, e), align_bytes=64)
-                dst, src = weave_views(woven[:], x_raw[g, c0][:, :, e * half : (e + 1) * half])
-                if e == 0:
-                    nc.vector.tensor_copy(out=dst, in_=src)
-                else:
-                    nc.scalar.copy(out=dst, in_=src)
-                parts.append(woven)
-            for e in range(2):
-                cols = slice(c0 + e * half, c0 + (e + 1) * half)
-                nc.vector.quantize_mx(
-                    out=x_words[g][:, cols].bitcast(FP8X4), scales=x_scales[PACK * g : P, cols], in_=parts[e][:]
-                )
+            load = max(q for gg, q in x_raw if gg == g and q <= c0)
+            last = g == PASSES - 1 and c0 + width == T
+            on_vector = width * (5 if last else 2) // 8
+            raw = x_raw[g, load][:, :, c0 - load : c0 - load + width]
+            woven = sb.tile([P, width * PACK], BF16, name="x_bf%d_%d" % (g, c0), align_bytes=64)
+            dst, src = weave_views(woven[:, : on_vector * PACK], raw[:, :, :on_vector])
+            nc.vector.tensor_copy(out=dst, in_=src)
+            dst, src = weave_views(woven[:, on_vector * PACK :], raw[:, :, on_vector:])
+            nc.scalar.copy(out=dst, in_=src)
+            cols = slice(c0, c0 + width)
+            nc.vector.quantize_mx(
+                out=x_words[g][:, cols].bitcast(FP8X4), scales=x_scales[PACK * g : P, cols], in_=woven[:]
+            )
 
         picked_words = {}
         picked_scales = {}
 
-        def gather_words(g, h):
-            picked_words[g, h] = sb.tile([P, HALF], U32, name="picked_words%d_%d" % (g, h), align_bytes=64)
-            nc.vector.tensor_copy(picked_words[g, h][:], x_words[g][:].indirect(offsets[:, 32 * h : 32 * (h + 1)]))
+        pick0 = starts(PICKS)
 
-        def gather_scales(h):
-            picked_scales[h] = sb.tile([P, HALF], U8, name="picked_scales%d" % h, align_bytes=64)
-            nc.vector.tensor_copy(picked_scales[h][:], x_scales[:].indirect(offsets[:, 32 * h : 32 * (h + 1)]))
+        def gather_words(g, h, tag=None):
+            name = "picked_words%d_%d" % (g, h)
+            picked_words[g, h] = sb.tile([P, PICKS[h]], U32, name=name, tag=tag or name, align_bytes=64)
+            entries = offsets[:, pick0[h] // 16 : (pick0[h] + PICKS[h]) // 16]
+            nc.vector.tensor_copy(picked_words[g, h][:], x_words[g][:].indirect(entries))
 
-        w1_bf = [sb.tile([P, PACK, P, PACK], BF16, name="w1_bf%d" % g, align_bytes=64) for g in range(PASSES)]
+        def gather_scales(h, tag=None):
+            name = "picked_scales%d" % h
+            picked_scales[h] = sb.tile([P, PICKS[h]], U8, name=name, tag=tag or name, align_bytes=64)
+            entries = offsets[:, pick0[h] // 16 : (pick0[h] + PICKS[h]) // 16]
+            nc.vector.tensor_copy(picked_scales[h][:], x_scales[:].indirect(entries))
+
+        w1_bf = [sb.tile([P, PACK, P, PACK], BF16, name="w1_bf%d" % g, tag="w1_bf%d" % g, align_bytes=64) for g in range(PASSES)]
         w1_words = [sb.tile([P, H], U32, name="w1_words%d" % g, align_bytes=64) for g in range(PASSES)]
         w1_scales = [sb.tile([P, H], U8, name="w1_scales%d" % g, align_bytes=64) for g in range(PASSES)]
 
         def weave_w1(g, a, engine_copy):
-            dst = w1_bf[g][:, :, a * 64 : (a + 1) * 64, :].rearrange("p t m j -> p m t j")
-            src = w1_raw[g, a][:].rearrange("p j (m t) -> p m t j", t=PACK)
+            dst = w1_bf[g][:, :, a * 64 : (a + 1) * 64, :].rearrange("p t m j -> p m j t")
+            src = w1_raw[g, a][:].rearrange("p j (m t) -> p m j t", t=PACK)
             engine_copy(out=dst, in_=src)
 
-        def quantise_w1(g):
-            for t in range(PACK):
-                cols = slice(t * P, (t + 1) * P)
+        def quantise_w1(g, pieces):
+            width = H // pieces
+            flat = w1_bf[g][:].rearrange("p t m j -> p (t m j)")
+            for c0 in range(0, H, width):
+                cols = slice(c0, c0 + width)
                 nc.vector.quantize_mx(
                     out=w1_words[g][:, cols].bitcast(FP8X4),
                     scales=w1_scales[g][:, cols],
-                    in_=w1_bf[g][:, t, :, :].rearrange("p m j -> p (m j)"),
+                    in_=flat[:, PACK * c0 : PACK * (c0 + width)],
                 )
 
-        acc = {}
+        def first_layer_pass(acc_ap, g, t, h, lo, width):
+            cols = slice(t * P, (t + 1) * P)
+            if g == 0:
+                words = first_words[:, pick0[h] + lo : pick0[h] + lo + width]
+            else:
+                words = picked_words[g, h][:, lo : lo + width]
+            nc.tensor.matmul_mx(
+                out=acc_ap,
+                lhsT=w1_words[g][:, cols].bitcast(FP8X4),
+                lhsT_scale=w1_scales[g][:, cols],
+                rhs=words.bitcast(FP8X4),
+                rhs_scale=picked_scales[h][PACK * g : P, lo : lo + width],
+                start=(g == 0),
+                stop=(g == PASSES - 1),
+            )
 
-        def first_layer(g, h):
-            for t in range(PACK):
-                if g == 0:
-                    acc[h, t] = psum.tile([P, HALF], F32, name="acc%d_%d" % (h, t), tag="bank%d" % (PACK * h + t))
-                cols = slice(t * P, (t + 1) * P)
-                nc.tensor.matmul_mx(
-                    out=acc[h, t][:],
-                    lhsT=w1_words[g][:, cols].bitcast(FP8X4),
-                    lhsT_scale=w1_scales[g][:, cols],
-                    rhs=picked_words[g, h][:].bitcast(FP8X4),
-                    rhs_scale=picked_scales[h][PACK * g : P, :],
-                    start=(g == 0),
-                    stop=(g == PASSES - 1),
-                )
+        def banks_for(first_bank, width):
+            per_bank = HALF // width
+            return [
+                psum.tile([P, per_bank, width], F32, name="acc%d" % b, tag="bank%d" % b)
+                for b in range(first_bank, first_bank + PACK // per_bank)
+            ]
 
-        for c0, width in zip(starts(X_CHUNKS[0]), X_CHUNKS[0]):
-            quantise_x(0, c0, width)
-        later = list(zip(starts(X_CHUNKS[1]), X_CHUNKS[1]))
-        quantise_x(1, *later[0])
-        gather_words(0, 0)
-        quantise_x(1, *later[1])
-        gather_words(0, 1)
-        for c0, width in later[2:]:
-            quantise_x(1, c0, width)
+        for c0 in range(0, T, UNIT):
+            quantise_x(0, c0, UNIT)
+        first_words = sb.tile([P, S], U32, name="picked_words0", align_bytes=64)
+        nc.vector.tensor_copy(first_words[:], x_words[0][:].indirect(offsets[:]))
+        for load, width in zip(starts(X_CHUNKS[1]), X_CHUNKS[1]):
+            for c0 in range(load, load + width, UNIT):
+                quantise_x(1, c0, min(width, UNIT))
 
         gather_scales(0)
         gather_words(1, 0)
         weave_w1(0, 0, nc.scalar.copy)
         weave_w1(0, 1, nc.scalar.copy)
-        gather_scales(1)
-        quantise_w1(0)
-        first_layer(0, 0)
-        gather_words(1, 1)
+        quantise_w1(0, 2)
+        acc = {0: banks_for(0, HALF)}
+        for t in range(PACK):
+            first_layer_pass(acc[0][t][:, 0, :], 0, t, 0, 0, HALF)
+        gather_words(1, 1, tag="w1_raw0_1")
+        gather_scales(1, tag="w1_bf0")
         weave_w1(1, 0, nc.scalar.copy)
-        weave_w1(1, 1, nc.vector.tensor_copy)
-        quantise_w1(1)
-        first_layer(1, 0)
-        first_layer(0, 1)
-        first_layer(1, 1)
+        gather_words(1, 2, tag="w1_raw1_0")
+        weave_w1(1, 1, nc.scalar.copy)
+        quantise_w1(1, 2)
+        for t in range(PACK):
+            first_layer_pass(acc[0][t][:, 0, :], 1, t, 0, 0, HALF)
+        gather_scales(2, tag="w1_bf1")
+        for s0, width, h, bank in ((512, 256, 1, 4), (768, 128, 2, 6), (896, 128, 2, 7)):
+            acc[s0] = banks_for(bank, width)
+            per_bank = HALF // width
+            for t in range(PACK):
+                for g in range(PASSES):
+                    first_layer_pass(acc[s0][t // per_bank][:, t % per_bank, :], g, t, h, s0 - pick0[h], width)
 
         w2_bf = sb.tile([P, N * PACK], BF16, name="w2_bf", align_bytes=64)
         w2_words = sb.tile([P, N], U32, name="w2_words", align_bytes=64)
@@ -166,50 +191,56 @@ def tile_picked_embpos_gelu_e_kernel(tc, xT, w1, w2, pos, offs, out):
         nc.scalar.copy(out=dst, in_=src)
 
         h_bf = {}
-        h_words = {}
-        h_scales = {}
+        h_words = sb.tile([P, S], U32, name="h_words", align_bytes=64)
+        h_scales = sb.tile([P, S], U8, name="h_scales", align_bytes=64)
 
         def hidden(s0, width):
-            h, off = divmod(s0, HALF)
+            a0 = max(q for q in acc if q <= s0)
             p0 = max(q for q in pos_sb if q <= s0)
             pre = sb.tile([P, PACK, width], F32, name="pre%d" % s0, align_bytes=64)
-            for t in range(PACK):
+            per_bank = PACK // len(acc[a0])
+            for b, bank in enumerate(acc[a0]):
+                ts = slice(b * per_bank, (b + 1) * per_bank)
                 nc.vector.tensor_tensor(
-                    pre[:, t, :], acc[h, t][:, off : off + width], pos_sb[p0][:, t, s0 - p0 : s0 - p0 + width], ADD
+                    pre[:, ts, :],
+                    bank[:, :, s0 - a0 : s0 - a0 + width],
+                    pos_sb[p0][:, ts, s0 - p0 : s0 - p0 + width],
+                    ADD,
                 )
             h_bf[s0] = sb.tile([P, width * PACK], BF16, name="h_bf%d" % s0, align_bytes=64)
             dst, src = weave_views(h_bf[s0][:], pre[:])
             nc.scalar.activation(dst, src, GELU)
 
         def quantise_h(s0, width):
-            h_words[s0] = sb.tile([P, width], U32, name="h_words%d" % s0, align_bytes=64)
-            h_scales[s0] = sb.tile([P, width], U8, name="h_scales%d" % s0, align_bytes=64)
-            nc.vector.quantize_mx(out=h_words[s0][:].bitcast(FP8X4), scales=h_scales[s0][:], in_=h_bf[s0][:])
+            cols = slice(s0, s0 + width)
+            nc.vector.quantize_mx(out=h_words[:, cols].bitcast(FP8X4), scales=h_scales[:, cols], in_=h_bf[s0][:])
 
         def second_layer(i, s0, width):
-            res = psum.tile([P, width], F32, name="res%d" % s0, tag="bank%d" % (i % PACK))
+            cols = slice(s0, s0 + width)
+            res = psum.tile([P, width], F32, name="res%d" % s0, tag="bank%d" % i)
             nc.tensor.matmul_mx(
                 out=res[:],
                 lhsT=w2_words[:].bitcast(FP8X4),
                 lhsT_scale=w2_scales[:],
-                rhs=h_words[s0][:].bitcast(FP8X4),
-                rhs_scale=h_scales[s0][:],
+                rhs=h_words[:, cols].bitcast(FP8X4),
+                rhs_scale=h_scales[:, cols],
                 start=True,
                 stop=True,
             )
             staged = sb.tile([P, width], F32, name="staged%d" % s0, align_bytes=64)
-            nc.scalar.copy(out=staged[:], in_=res[:])
-            nc.sync.dma_start(out=out[:, s0 : s0 + width], in_=staged[:])
+            if i == 0:
+                nc.vector.tensor_copy(out=staged[:], in_=res[:])
+            else:
+                nc.scalar.copy(out=staged[:], in_=res[:])
+            nc.sync.dma_start(out=out[:, cols], in_=staged[:])
 
         chunks = list(zip(starts(H_CHUNKS), H_CHUNKS))
         for i, (s0, width) in enumerate(chunks):
             hidden(s0, width)
-            if i == 0:
-                nc.vector.quantize_mx(out=w2_words[:].bitcast(FP8X4), scales=w2_scales[:], in_=w2_bf[:])
             if i >= 1:
                 quantise_h(*chunks[i - 1])
-            if i >= 3:
-                second_layer(i - 3, *chunks[i - 3])
+            if i == 1:
+                nc.vector.quantize_mx(out=w2_words[:].bitcast(FP8X4), scales=w2_scales[:], in_=w2_bf[:])
         quantise_h(*chunks[-1])
-        for i in range(len(chunks) - 3, len(chunks)):
-            second_layer(i, *chunks[i])
+        for i, (s0, width) in enumerate(zip(starts(OUT_CHUNKS), OUT_CHUNKS)):
+            second_layer(i, s0, width)

@@ -22,10 +22,10 @@ PASSES = K // K_PASS
 HALF = 512
 X_CHUNKS = ((1024, 512, 512), (512, 512, 512, 256, 256))
 UNIT = 512
-POS_CHUNKS = (512, 512)
+POS_CHUNKS = (512, 256, 256)
 PICKS = (512, 256, 256)
-H_CHUNKS = (256, 256, 256, 128, 128)
-OUT_CHUNKS = (512, 256, 128, 128)
+H_CHUNKS = (128, 128, 256, 256, 128, 128)
+OUT_CHUNKS = (256, 256, 256, 128, 128)
 
 
 def starts(widths):
@@ -228,19 +228,18 @@ def tile_picked_embpos_gelu_e_kernel(tc, xT, w1, w2, pos, offs, out):
                 stop=True,
             )
             staged = sb.tile([P, width], F32, name="staged%d" % s0, align_bytes=64)
-            if i == 0:
-                nc.vector.tensor_copy(out=staged[:], in_=res[:])
-            else:
-                nc.scalar.copy(out=staged[:], in_=res[:])
+            nc.scalar.copy(out=staged[:], in_=res[:])
             nc.sync.dma_start(out=out[:, cols], in_=staged[:])
 
         chunks = list(zip(starts(H_CHUNKS), H_CHUNKS))
-        for i, (s0, width) in enumerate(chunks):
-            hidden(s0, width)
-            if i >= 1:
-                quantise_h(*chunks[i - 1])
+        outs = {s0 + width: (i, s0, width) for i, (s0, width) in enumerate(zip(starts(OUT_CHUNKS), OUT_CHUNKS))}
+
+        for i, (s0, width) in enumerate(chunks + [(S, 0), (S, 0), (S, 0)]):
+            if width:
+                hidden(s0, width)
             if i == 1:
                 nc.vector.quantize_mx(out=w2_words[:].bitcast(FP8X4), scales=w2_scales[:], in_=w2_bf[:])
-        quantise_h(*chunks[-1])
-        for i, (s0, width) in enumerate(zip(starts(OUT_CHUNKS), OUT_CHUNKS)):
-            second_layer(i, s0, width)
+            if 2 <= i < len(chunks) + 2:
+                quantise_h(*chunks[i - 2])
+            if i >= 3 and sum(chunks[i - 3]) in outs:
+                second_layer(*outs[sum(chunks[i - 3])])

@@ -19,23 +19,30 @@ P = 128
 PACK = 4
 K_PASS = P * PACK
 PASSES = K // K_PASS
-HALF = 512
-X_CHUNKS = ((1024, 512, 512), (512, 512, 512, 256, 256))
-UNIT = 512
-POS_CHUNKS = (512, 256, 256)
+BANK = 512
+LIST_ROWS = 16
+ALIGN = 64
+
+X_LOADS = ((1024, 512, 512), (512, 512, 512, 256, 128, 128))
+X_UNIT = 512
+VECTOR_EIGHTHS, VECTOR_EIGHTHS_LAST = 2, 5
+W1_HALVES = 2
+POS_LOADS = (256, 256, 256, 256)
 PICKS = (512, 256, 256)
-H_CHUNKS = (128, 128, 256, 256, 128, 128)
-OUT_CHUNKS = (256, 256, 256, 128, 128)
+LATE_GROUPS = ((512, 256, 1, 4), (768, 128, 2, 6), (896, 128, 2, 7))
+H_STEPS = (128, 128, 256, 256, 128, 128)
+OUT_STEPS = (256, 256, 256, 128, 128)
+QUANTISE_LAG, OUT_LAG = 2, 3
 
 
-def starts(widths):
-    return [sum(widths[:i]) for i in range(len(widths))]
+def spans(widths):
+    return [(sum(widths[:i]), width) for i, width in enumerate(widths)]
 
 
 def weave_views(dst, src):
     return (
-        dst.rearrange("p (c i t) -> p c t i", i=4, t=PACK),
-        src.rearrange("p t (c i) -> p c t i", i=4),
+        dst.rearrange("p (c i j) -> p c j i", i=4, j=PACK),
+        src.rearrange("p j (c i) -> p c j i", i=4),
     )
 
 
@@ -46,43 +53,45 @@ def tile_picked_embpos_gelu_e_kernel(tc, xT, w1, w2, pos, offs, out):
         sb = ctx.enter_context(tc.tile_pool(name="sb", bufs=1))
         psum = ctx.enter_context(tc.psum_pool(name="psum", bufs=1))
 
-        offsets = lists.tile([P, S // 16], U16, name="offsets")
-        x_scales = sb.tile([P, T], U8, name="x_scales", align_bytes=64)
+        offsets = lists.tile([P, S // LIST_ROWS], U16, name="offsets")
+        x_scales = sb.tile([P, T], U8, name="x_scales", align_bytes=ALIGN)
         nc.vector.memset(x_scales[:].bitcast(I32), 0)
         warm = sb.tile([P, 2], F32, name="warm")
-        nc.vector.memset(warm[:, 0:1], 0.0)
+        nc.gpsimd.memset(warm[:, 0:1], 0.0)
         nc.scalar.activation(warm[:, 1:2], warm[:, 0:1], GELU)
-        x_words = [sb.tile([P, T], U32, name="x_words%d" % g, align_bytes=64) for g in range(PASSES)]
+        x_words = [sb.tile([P, T], U32, name="x_words%d" % g, align_bytes=ALIGN) for g in range(PASSES)]
 
         x_raw = {}
         for g in range(PASSES):
             rows = xT[g * K_PASS : (g + 1) * K_PASS, :].rearrange("(p j) c -> p j c", j=PACK)
-            for c0, width in zip(starts(X_CHUNKS[g]), X_CHUNKS[g]):
-                x_raw[g, c0] = sb.tile([P, PACK, width], F32, name="x_raw%d_%d" % (g, c0), align_bytes=64)
+            for c0, width in spans(X_LOADS[g]):
+                x_raw[g, c0] = sb.tile([P, PACK, width], F32, name="x_raw%d_%d" % (g, c0), align_bytes=ALIGN)
                 nc.sync.dma_start(out=x_raw[g, c0][:], in_=rows[:, :, c0 : c0 + width])
             if g == 0:
                 nc.sync.dma_start(offsets[:], offs)
         w1_raw = {}
+        channels = H // W1_HALVES
         for g in range(PASSES):
             rows = w1[g * K_PASS : (g + 1) * K_PASS, :].rearrange("(p j) c -> p j c", j=PACK)
-            for a in range(2):
-                w1_raw[g, a] = sb.tile([P, PACK, H // 2], F32, name="w1_raw%d_%d" % (g, a), tag="w1_raw%d_%d" % (g, a), align_bytes=64)
-                nc.sync.dma_start(out=w1_raw[g, a][:], in_=rows[:, :, a * (H // 2) : (a + 1) * (H // 2)])
+            for a in range(W1_HALVES):
+                name = "w1_raw%d_%d" % (g, a)
+                w1_raw[g, a] = sb.tile([P, PACK, channels], F32, name=name, tag=name, align_bytes=ALIGN)
+                nc.sync.dma_start(out=w1_raw[g, a][:], in_=rows[:, :, a * channels : (a + 1) * channels])
         pos_rows = pos.rearrange("(p t) s -> p t s", t=PACK)
         pos_sb = {}
-        w2_raw = sb.tile([P, PACK, N], F32, name="w2_raw", align_bytes=64)
-        for s0, width in zip(starts(POS_CHUNKS), POS_CHUNKS):
-            pos_sb[s0] = sb.tile([P, PACK, width], F32, name="pos%d" % s0, align_bytes=64)
+        w2_raw = sb.tile([P, PACK, N], F32, name="w2_raw", align_bytes=ALIGN)
+        for s0, width in spans(POS_LOADS):
+            pos_sb[s0] = sb.tile([P, PACK, width], F32, name="pos%d" % s0, align_bytes=ALIGN)
             nc.sync.dma_start(out=pos_sb[s0][:], in_=pos_rows[:, :, s0 : s0 + width])
             if s0 == 0:
                 nc.sync.dma_start(out=w2_raw[:], in_=w2.rearrange("(p j) n -> p j n", j=PACK))
 
         def quantise_x(g, c0, width):
-            load = max(q for gg, q in x_raw if gg == g and q <= c0)
+            load0 = max(start for pass_of, start in x_raw if pass_of == g and start <= c0)
             last = g == PASSES - 1 and c0 + width == T
-            on_vector = width * (5 if last else 2) // 8
-            raw = x_raw[g, load][:, :, c0 - load : c0 - load + width]
-            woven = sb.tile([P, width * PACK], BF16, name="x_bf%d_%d" % (g, c0), align_bytes=64)
+            on_vector = width * (VECTOR_EIGHTHS_LAST if last else VECTOR_EIGHTHS) // 8
+            raw = x_raw[g, load0][:, :, c0 - load0 : c0 - load0 + width]
+            woven = sb.tile([P, width * PACK], BF16, name="x_bf%d_%d" % (g, c0), align_bytes=ALIGN)
             dst, src = weave_views(woven[:, : on_vector * PACK], raw[:, :, :on_vector])
             nc.vector.tensor_copy(out=dst, in_=src)
             dst, src = weave_views(woven[:, on_vector * PACK :], raw[:, :, on_vector:])
@@ -92,122 +101,122 @@ def tile_picked_embpos_gelu_e_kernel(tc, xT, w1, w2, pos, offs, out):
                 out=x_words[g][:, cols].bitcast(FP8X4), scales=x_scales[PACK * g : P, cols], in_=woven[:]
             )
 
-        picked_words = {}
+        picks = spans(PICKS)
+        second_words = {}
         picked_scales = {}
 
-        pick0 = starts(PICKS)
+        def gather(window, piece, dtype, name, tag):
+            s0, width = picks[piece]
+            picked = sb.tile([P, width], dtype, name=name, tag=tag or name, align_bytes=ALIGN)
+            entries = offsets[:, s0 // LIST_ROWS : (s0 + width) // LIST_ROWS]
+            nc.vector.tensor_copy(picked[:], window[:].indirect(entries))
+            return picked
 
-        def gather_words(g, h, tag=None):
-            name = "picked_words%d_%d" % (g, h)
-            picked_words[g, h] = sb.tile([P, PICKS[h]], U32, name=name, tag=tag or name, align_bytes=64)
-            entries = offsets[:, pick0[h] // 16 : (pick0[h] + PICKS[h]) // 16]
-            nc.vector.tensor_copy(picked_words[g, h][:], x_words[g][:].indirect(entries))
+        def gather_second_words(piece, tag=None):
+            second_words[piece] = gather(x_words[1], piece, U32, "picked_words1_%d" % piece, tag)
 
-        def gather_scales(h, tag=None):
-            name = "picked_scales%d" % h
-            picked_scales[h] = sb.tile([P, PICKS[h]], U8, name=name, tag=tag or name, align_bytes=64)
-            entries = offsets[:, pick0[h] // 16 : (pick0[h] + PICKS[h]) // 16]
-            nc.vector.tensor_copy(picked_scales[h][:], x_scales[:].indirect(entries))
+        def gather_scales(piece, tag=None):
+            picked_scales[piece] = gather(x_scales, piece, U8, "picked_scales%d" % piece, tag)
 
-        w1_bf = [sb.tile([P, PACK, P, PACK], BF16, name="w1_bf%d" % g, tag="w1_bf%d" % g, align_bytes=64) for g in range(PASSES)]
-        w1_words = [sb.tile([P, H], U32, name="w1_words%d" % g, align_bytes=64) for g in range(PASSES)]
-        w1_scales = [sb.tile([P, H], U8, name="w1_scales%d" % g, align_bytes=64) for g in range(PASSES)]
+        w1_bf = [
+            sb.tile([P, PACK, P, PACK], BF16, name="w1_bf%d" % g, tag="w1_bf%d" % g, align_bytes=ALIGN)
+            for g in range(PASSES)
+        ]
+        w1_words = [sb.tile([P, H], U32, name="w1_words%d" % g, align_bytes=ALIGN) for g in range(PASSES)]
+        w1_scales = [sb.tile([P, H], U8, name="w1_scales%d" % g, align_bytes=ALIGN) for g in range(PASSES)]
 
-        def weave_w1(g, a, engine_copy):
-            dst = w1_bf[g][:, :, a * 64 : (a + 1) * 64, :].rearrange("p t m j -> p m j t")
+        def weave_w1(g, a):
+            ms = slice(a * (P // W1_HALVES), (a + 1) * (P // W1_HALVES))
+            dst = w1_bf[g][:, :, ms, :].rearrange("p t m j -> p m j t")
             src = w1_raw[g, a][:].rearrange("p j (m t) -> p m j t", t=PACK)
-            engine_copy(out=dst, in_=src)
+            nc.scalar.copy(out=dst, in_=src)
 
-        def quantise_w1(g, pieces):
-            width = H // pieces
+        def quantise_w1(g):
             flat = w1_bf[g][:].rearrange("p t m j -> p (t m j)")
-            for c0 in range(0, H, width):
-                cols = slice(c0, c0 + width)
+            for c0 in range(0, H, channels):
+                cols = slice(c0, c0 + channels)
                 nc.vector.quantize_mx(
                     out=w1_words[g][:, cols].bitcast(FP8X4),
                     scales=w1_scales[g][:, cols],
-                    in_=flat[:, PACK * c0 : PACK * (c0 + width)],
+                    in_=flat[:, PACK * c0 : PACK * (c0 + channels)],
                 )
 
-        def first_layer_pass(acc_ap, g, t, h, lo, width):
+        def first_product_pass(acc_ap, g, t, piece, s0, width):
             cols = slice(t * P, (t + 1) * P)
-            if g == 0:
-                words = first_words[:, pick0[h] + lo : pick0[h] + lo + width]
-            else:
-                words = picked_words[g, h][:, lo : lo + width]
+            in_piece = slice(s0 - picks[piece][0], s0 - picks[piece][0] + width)
+            words = first_words[:, s0 : s0 + width] if g == 0 else second_words[piece][:, in_piece]
             nc.tensor.matmul_mx(
                 out=acc_ap,
                 lhsT=w1_words[g][:, cols].bitcast(FP8X4),
                 lhsT_scale=w1_scales[g][:, cols],
                 rhs=words.bitcast(FP8X4),
-                rhs_scale=picked_scales[h][PACK * g : P, lo : lo + width],
+                rhs_scale=picked_scales[piece][PACK * g : P, in_piece],
                 start=(g == 0),
                 stop=(g == PASSES - 1),
             )
 
         def banks_for(first_bank, width):
-            per_bank = HALF // width
+            per_bank = BANK // width
             return [
                 psum.tile([P, per_bank, width], F32, name="acc%d" % b, tag="bank%d" % b)
                 for b in range(first_bank, first_bank + PACK // per_bank)
             ]
 
-        for c0 in range(0, T, UNIT):
-            quantise_x(0, c0, UNIT)
-        first_words = sb.tile([P, S], U32, name="picked_words0", align_bytes=64)
+        for c0 in range(0, T, X_UNIT):
+            quantise_x(0, c0, X_UNIT)
+        first_words = sb.tile([P, S], U32, name="picked_words0", align_bytes=ALIGN)
         nc.vector.tensor_copy(first_words[:], x_words[0][:].indirect(offsets[:]))
-        for load, width in zip(starts(X_CHUNKS[1]), X_CHUNKS[1]):
-            for c0 in range(load, load + width, UNIT):
-                quantise_x(1, c0, min(width, UNIT))
+        for c0, width in spans(X_LOADS[1]):
+            quantise_x(1, c0, width)
 
         gather_scales(0)
-        gather_words(1, 0)
-        weave_w1(0, 0, nc.scalar.copy)
-        weave_w1(0, 1, nc.scalar.copy)
-        quantise_w1(0, 2)
-        acc = {0: banks_for(0, HALF)}
+        gather_second_words(0)
+        weave_w1(0, 0)
+        weave_w1(0, 1)
+        quantise_w1(0)
+        acc = {0: banks_for(0, PICKS[0])}
         for t in range(PACK):
-            first_layer_pass(acc[0][t][:, 0, :], 0, t, 0, 0, HALF)
-        gather_words(1, 1, tag="w1_raw0_1")
+            first_product_pass(acc[0][t][:, 0, :], 0, t, 0, 0, PICKS[0])
+        gather_second_words(1, tag="w1_raw0_1")
         gather_scales(1, tag="w1_bf0")
-        weave_w1(1, 0, nc.scalar.copy)
-        gather_words(1, 2, tag="w1_raw1_0")
-        weave_w1(1, 1, nc.scalar.copy)
-        quantise_w1(1, 2)
+        weave_w1(1, 0)
+        gather_second_words(2, tag="w1_raw1_0")
+        weave_w1(1, 1)
+        quantise_w1(1)
         for t in range(PACK):
-            first_layer_pass(acc[0][t][:, 0, :], 1, t, 0, 0, HALF)
+            first_product_pass(acc[0][t][:, 0, :], 1, t, 0, 0, PICKS[0])
         gather_scales(2, tag="w1_bf1")
-        for s0, width, h, bank in ((512, 256, 1, 4), (768, 128, 2, 6), (896, 128, 2, 7)):
-            acc[s0] = banks_for(bank, width)
-            per_bank = HALF // width
+        for s0, width, piece, first_bank in LATE_GROUPS:
+            acc[s0] = banks_for(first_bank, width)
+            per_bank = BANK // width
             for t in range(PACK):
                 for g in range(PASSES):
-                    first_layer_pass(acc[s0][t // per_bank][:, t % per_bank, :], g, t, h, s0 - pick0[h], width)
+                    first_product_pass(acc[s0][t // per_bank][:, t % per_bank, :], g, t, piece, s0, width)
 
-        w2_bf = sb.tile([P, N * PACK], BF16, name="w2_bf", align_bytes=64)
-        w2_words = sb.tile([P, N], U32, name="w2_words", align_bytes=64)
-        w2_scales = sb.tile([P, N], U8, name="w2_scales", align_bytes=64)
+        w2_bf = sb.tile([P, N * PACK], BF16, name="w2_bf", align_bytes=ALIGN)
+        w2_words = sb.tile([P, N], U32, name="w2_words", align_bytes=ALIGN)
+        w2_scales = sb.tile([P, N], U8, name="w2_scales", align_bytes=ALIGN)
         dst, src = weave_views(w2_bf[:], w2_raw[:])
         nc.scalar.copy(out=dst, in_=src)
 
         h_bf = {}
-        h_words = sb.tile([P, S], U32, name="h_words", align_bytes=64)
-        h_scales = sb.tile([P, S], U8, name="h_scales", align_bytes=64)
+        h_words = sb.tile([P, S], U32, name="h_words", align_bytes=ALIGN)
+        h_scales = sb.tile([P, S], U8, name="h_scales", align_bytes=ALIGN)
 
         def hidden(s0, width):
-            a0 = max(q for q in acc if q <= s0)
-            p0 = max(q for q in pos_sb if q <= s0)
-            pre = sb.tile([P, PACK, width], F32, name="pre%d" % s0, align_bytes=64)
-            per_bank = PACK // len(acc[a0])
-            for b, bank in enumerate(acc[a0]):
+            acc0 = max(start for start in acc if start <= s0)
+            pos0 = max(start for start in pos_sb if start <= s0)
+            pre = sb.tile([P, PACK, width], F32, name="pre%d" % s0, align_bytes=ALIGN)
+            per_bank = PACK // len(acc[acc0])
+            for b, bank in enumerate(acc[acc0]):
                 ts = slice(b * per_bank, (b + 1) * per_bank)
                 nc.vector.tensor_tensor(
                     pre[:, ts, :],
-                    bank[:, :, s0 - a0 : s0 - a0 + width],
-                    pos_sb[p0][:, ts, s0 - p0 : s0 - p0 + width],
+                    bank[:, :, s0 - acc0 : s0 - acc0 + width],
+                    pos_sb[pos0][:, ts, s0 - pos0 : s0 - pos0 + width],
                     ADD,
                 )
-            h_bf[s0] = sb.tile([P, width * PACK], BF16, name="h_bf%d" % s0, align_bytes=64)
+            h_bf[s0] = sb.tile([P, width * PACK], BF16, name="h_bf%d" % s0, align_bytes=ALIGN)
             dst, src = weave_views(h_bf[s0][:], pre[:])
             nc.scalar.activation(dst, src, GELU)
 
@@ -215,9 +224,9 @@ def tile_picked_embpos_gelu_e_kernel(tc, xT, w1, w2, pos, offs, out):
             cols = slice(s0, s0 + width)
             nc.vector.quantize_mx(out=h_words[:, cols].bitcast(FP8X4), scales=h_scales[:, cols], in_=h_bf[s0][:])
 
-        def second_layer(i, s0, width):
+        def second_product(b, s0, width):
             cols = slice(s0, s0 + width)
-            res = psum.tile([P, width], F32, name="res%d" % s0, tag="bank%d" % i)
+            res = psum.tile([P, width], F32, name="res%d" % s0, tag="bank%d" % b)
             nc.tensor.matmul_mx(
                 out=res[:],
                 lhsT=w2_words[:].bitcast(FP8X4),
@@ -227,19 +236,18 @@ def tile_picked_embpos_gelu_e_kernel(tc, xT, w1, w2, pos, offs, out):
                 start=True,
                 stop=True,
             )
-            staged = sb.tile([P, width], F32, name="staged%d" % s0, align_bytes=64)
+            staged = sb.tile([P, width], F32, name="staged%d" % s0, align_bytes=ALIGN)
             nc.scalar.copy(out=staged[:], in_=res[:])
             nc.sync.dma_start(out=out[:, cols], in_=staged[:])
 
-        chunks = list(zip(starts(H_CHUNKS), H_CHUNKS))
-        outs = {s0 + width: (i, s0, width) for i, (s0, width) in enumerate(zip(starts(OUT_CHUNKS), OUT_CHUNKS))}
-
-        for i, (s0, width) in enumerate(chunks + [(S, 0), (S, 0), (S, 0)]):
-            if width:
-                hidden(s0, width)
-            if i == 1:
+        steps = spans(H_STEPS)
+        outs_by_end = {s0 + width: (b, s0, width) for b, (s0, width) in enumerate(spans(OUT_STEPS))}
+        for i in range(len(steps) + OUT_LAG):
+            if i < len(steps):
+                hidden(*steps[i])
+            if i == QUANTISE_LAG - 1:
                 nc.vector.quantize_mx(out=w2_words[:].bitcast(FP8X4), scales=w2_scales[:], in_=w2_bf[:])
-            if 2 <= i < len(chunks) + 2:
-                quantise_h(*chunks[i - 2])
-            if i >= 3 and sum(chunks[i - 3]) in outs:
-                second_layer(*outs[sum(chunks[i - 3])])
+            if 0 <= i - QUANTISE_LAG < len(steps):
+                quantise_h(*steps[i - QUANTISE_LAG])
+            if i >= OUT_LAG and sum(steps[i - OUT_LAG]) in outs_by_end:
+                second_product(*outs_by_end[sum(steps[i - OUT_LAG])])

@@ -23,16 +23,20 @@ BANK = 512
 LIST_ROWS = 16
 ALIGN = 64
 
-X_LOADS = ((1024, 512, 512), (512, 512, 512, 256, 128, 128))
+X_PLAN = (
+    (((512, 3), (512, 3), (256, 4)), ((512, 5), (256, 5))),
+    (((512, 4), (512, 3)), ((512, 4),), ((256, 4),), ((256, 5),)),
+)
+X_LOADS = tuple(tuple(sum(width for width, share in load) for load in loads) for loads in X_PLAN)
 X_UNIT = 512
-VECTOR_EIGHTHS, VECTOR_EIGHTHS_LAST = 2, 5
 W1_HALVES = 2
-POS_LOADS = (256, 256, 256, 256)
-PICKS = (512, 256, 256)
-LATE_GROUPS = ((512, 256, 1, 4), (768, 128, 2, 6), (896, 128, 2, 7))
-H_STEPS = (128, 128, 256, 256, 128, 128)
+W1_LAST_ON_VECTOR = 16
+POS_LOADS = (512, 256, 256)
+PICKS = (256, 256, 256, 256)
+H_STEPS = (128,) * 8
 OUT_STEPS = (256, 256, 256, 128, 128)
-QUANTISE_LAG, OUT_LAG = 2, 3
+H_WORDS_PLACES = ("pos0", "pre640", None, None, None)
+COPIES_ON_VECTOR = (0, 3)
 
 
 def spans(widths):
@@ -81,21 +85,21 @@ def tile_picked_embpos_gelu_e_kernel(tc, xT, w1, w2, pos, offs, out):
         pos_sb = {}
         w2_raw = sb.tile([P, PACK, N], F32, name="w2_raw", align_bytes=ALIGN)
         for s0, width in spans(POS_LOADS):
-            pos_sb[s0] = sb.tile([P, PACK, width], F32, name="pos%d" % s0, align_bytes=ALIGN)
+            pos_sb[s0] = sb.tile([P, PACK, width], F32, name="pos%d" % s0, tag="pos%d" % s0, align_bytes=ALIGN)
             nc.sync.dma_start(out=pos_sb[s0][:], in_=pos_rows[:, :, s0 : s0 + width])
             if s0 == 0:
                 nc.sync.dma_start(out=w2_raw[:], in_=w2.rearrange("(p j) n -> p j n", j=PACK))
 
-        def quantise_x(g, c0, width):
+        def quantise_x(g, c0, width, eighths):
             load0 = max(start for pass_of, start in x_raw if pass_of == g and start <= c0)
-            last = g == PASSES - 1 and c0 + width == T
-            on_vector = width * (VECTOR_EIGHTHS_LAST if last else VECTOR_EIGHTHS) // 8
+            on_vector = width * eighths // 8
             raw = x_raw[g, load0][:, :, c0 - load0 : c0 - load0 + width]
             woven = sb.tile([P, width * PACK], BF16, name="x_bf%d_%d" % (g, c0), align_bytes=ALIGN)
             dst, src = weave_views(woven[:, : on_vector * PACK], raw[:, :, :on_vector])
             nc.vector.tensor_copy(out=dst, in_=src)
-            dst, src = weave_views(woven[:, on_vector * PACK :], raw[:, :, on_vector:])
-            nc.scalar.copy(out=dst, in_=src)
+            if on_vector < width:
+                dst, src = weave_views(woven[:, on_vector * PACK :], raw[:, :, on_vector:])
+                nc.scalar.copy(out=dst, in_=src)
             cols = slice(c0, c0 + width)
             nc.vector.quantize_mx(
                 out=x_words[g][:, cols].bitcast(FP8X4), scales=x_scales[PACK * g : P, cols], in_=woven[:]
@@ -103,20 +107,16 @@ def tile_picked_embpos_gelu_e_kernel(tc, xT, w1, w2, pos, offs, out):
 
         picks = spans(PICKS)
         second_words = {}
-        picked_scales = {}
 
-        def gather(window, piece, dtype, name, tag):
-            s0, width = picks[piece]
+        def gather(window, s0, width, dtype, name, tag):
             picked = sb.tile([P, width], dtype, name=name, tag=tag or name, align_bytes=ALIGN)
             entries = offsets[:, s0 // LIST_ROWS : (s0 + width) // LIST_ROWS]
             nc.vector.tensor_copy(picked[:], window[:].indirect(entries))
             return picked
 
         def gather_second_words(piece, tag=None):
-            second_words[piece] = gather(x_words[1], piece, U32, "picked_words1_%d" % piece, tag)
+            second_words[piece] = gather(x_words[1], *picks[piece], U32, "picked_words1_%d" % piece, tag)
 
-        def gather_scales(piece, tag=None):
-            picked_scales[piece] = gather(x_scales, piece, U8, "picked_scales%d" % piece, tag)
 
         w1_bf = [
             sb.tile([P, PACK, P, PACK], BF16, name="w1_bf%d" % g, tag="w1_bf%d" % g, align_bytes=ALIGN)
@@ -129,16 +129,19 @@ def tile_picked_embpos_gelu_e_kernel(tc, xT, w1, w2, pos, offs, out):
             ms = slice(a * (P // W1_HALVES), (a + 1) * (P // W1_HALVES))
             dst = w1_bf[g][:, :, ms, :].rearrange("p t m j -> p m j t")
             src = w1_raw[g, a][:].rearrange("p j (m t) -> p m j t", t=PACK)
-            nc.scalar.copy(out=dst, in_=src)
+            split = W1_LAST_ON_VECTOR if (g, a) == (PASSES - 1, W1_HALVES - 1) else 0
+            if split:
+                nc.vector.tensor_copy(out=dst[:, :split], in_=src[:, :split])
+            nc.scalar.copy(out=dst[:, split:], in_=src[:, split:])
 
         def quantise_w1(g):
             flat = w1_bf[g][:].rearrange("p t m j -> p (t m j)")
-            for c0 in range(0, H, channels):
-                cols = slice(c0, c0 + channels)
+            for c0 in range(0, H, P):
+                cols = slice(c0, c0 + P)
                 nc.vector.quantize_mx(
                     out=w1_words[g][:, cols].bitcast(FP8X4),
                     scales=w1_scales[g][:, cols],
-                    in_=flat[:, PACK * c0 : PACK * (c0 + channels)],
+                    in_=flat[:, PACK * c0 : PACK * (c0 + P)],
                 )
 
         def first_product_pass(acc_ap, g, t, piece, s0, width):
@@ -150,48 +153,56 @@ def tile_picked_embpos_gelu_e_kernel(tc, xT, w1, w2, pos, offs, out):
                 lhsT=w1_words[g][:, cols].bitcast(FP8X4),
                 lhsT_scale=w1_scales[g][:, cols],
                 rhs=words.bitcast(FP8X4),
-                rhs_scale=picked_scales[piece][PACK * g : P, in_piece],
+                rhs_scale=picked_scales[s0 // (S // 2)][PACK * g : P, s0 % (S // 2) : s0 % (S // 2) + width],
                 start=(g == 0),
                 stop=(g == PASSES - 1),
             )
 
-        def banks_for(first_bank, width):
-            per_bank = BANK // width
+        def banks_for(first_bank, width, per_bank):
             return [
                 psum.tile([P, per_bank, width], F32, name="acc%d" % b, tag="bank%d" % b)
                 for b in range(first_bank, first_bank + PACK // per_bank)
             ]
 
-        for c0 in range(0, T, X_UNIT):
-            quantise_x(0, c0, X_UNIT)
+        def quantise_pass(g):
+            units = [unit for load in X_PLAN[g] for unit in load]
+            for (c0, width), (same, eighths) in zip(spans([width for width, eighths in units]), units):
+                quantise_x(g, c0, width, eighths)
+
+        quantise_pass(0)
         first_words = sb.tile([P, S], U32, name="picked_words0", align_bytes=ALIGN)
         nc.vector.tensor_copy(first_words[:], x_words[0][:].indirect(offsets[:]))
-        for c0, width in spans(X_LOADS[1]):
-            quantise_x(1, c0, width)
+        quantise_pass(1)
 
-        gather_scales(0)
+        picked_scales = {0: gather(x_scales, 0, S // 2, U8, "picked_scales0", None)}
         gather_second_words(0)
+        gather_second_words(1)
         weave_w1(0, 0)
         weave_w1(0, 1)
         quantise_w1(0)
-        acc = {0: banks_for(0, PICKS[0])}
-        for t in range(PACK):
-            first_product_pass(acc[0][t][:, 0, :], 0, t, 0, 0, PICKS[0])
-        gather_second_words(1, tag="w1_raw0_1")
-        gather_scales(1, tag="w1_bf0")
+        acc = {picks[0][0]: banks_for(0, PICKS[0], 1), picks[1][0]: banks_for(PACK, PICKS[1], 1)}
+
+        def open_pieces_pass(g):
+            for piece in range(2):
+                s0, width = picks[piece]
+                for t in range(PACK):
+                    first_product_pass(acc[s0][t][:, 0, :], g, t, piece, s0, width)
+
+        open_pieces_pass(0)
+        picked_scales[1] = gather(x_scales, S // 2, S // 2, U8, "picked_scales1", "w1_bf0")
         weave_w1(1, 0)
         gather_second_words(2, tag="w1_raw1_0")
         weave_w1(1, 1)
         quantise_w1(1)
-        for t in range(PACK):
-            first_product_pass(acc[0][t][:, 0, :], 1, t, 0, 0, PICKS[0])
-        gather_scales(2, tag="w1_bf1")
-        for s0, width, piece, first_bank in LATE_GROUPS:
-            acc[s0] = banks_for(first_bank, width)
-            per_bank = BANK // width
-            for t in range(PACK):
-                for g in range(PASSES):
-                    first_product_pass(acc[s0][t // per_bank][:, t % per_bank, :], g, t, piece, s0, width)
+        open_pieces_pass(1)
+        gather_second_words(3, tag="w1_bf1")
+
+        def late_pieces():
+            for b, s0 in enumerate(range(picks[2][0], S, P)):
+                acc[s0] = banks_for(b, P, PACK)
+                for t in range(PACK):
+                    for g in range(PASSES):
+                        first_product_pass(acc[s0][0][:, t, :], g, t, 2 + b // 2, s0, P)
 
         w2_bf = sb.tile([P, N * PACK], BF16, name="w2_bf", align_bytes=ALIGN)
         w2_words = sb.tile([P, N], U32, name="w2_words", align_bytes=ALIGN)
@@ -199,14 +210,14 @@ def tile_picked_embpos_gelu_e_kernel(tc, xT, w1, w2, pos, offs, out):
         dst, src = weave_views(w2_bf[:], w2_raw[:])
         nc.scalar.copy(out=dst, in_=src)
 
-        h_bf = {}
-        h_words = sb.tile([P, S], U32, name="h_words", align_bytes=ALIGN)
+        h_bf = sb.tile([P, S * PACK], BF16, name="h_bf", align_bytes=ALIGN)
+        h_words = {}
         h_scales = sb.tile([P, S], U8, name="h_scales", align_bytes=ALIGN)
 
         def hidden(s0, width):
             acc0 = max(start for start in acc if start <= s0)
             pos0 = max(start for start in pos_sb if start <= s0)
-            pre = sb.tile([P, PACK, width], F32, name="pre%d" % s0, align_bytes=ALIGN)
+            pre = sb.tile([P, PACK, width], F32, name="pre%d" % s0, tag="pre%d" % s0, align_bytes=ALIGN)
             per_bank = PACK // len(acc[acc0])
             for b, bank in enumerate(acc[acc0]):
                 ts = slice(b * per_bank, (b + 1) * per_bank)
@@ -216,38 +227,44 @@ def tile_picked_embpos_gelu_e_kernel(tc, xT, w1, w2, pos, offs, out):
                     pos_sb[pos0][:, ts, s0 - pos0 : s0 - pos0 + width],
                     ADD,
                 )
-            h_bf[s0] = sb.tile([P, width * PACK], BF16, name="h_bf%d" % s0, align_bytes=ALIGN)
-            dst, src = weave_views(h_bf[s0][:], pre[:])
+            dst, src = weave_views(h_bf[:, PACK * s0 : PACK * (s0 + width)], pre[:])
             nc.scalar.activation(dst, src, GELU)
 
-        def quantise_h(s0, width):
-            cols = slice(s0, s0 + width)
-            nc.vector.quantize_mx(out=h_words[:, cols].bitcast(FP8X4), scales=h_scales[:, cols], in_=h_bf[s0][:])
+        def quantise_h(s0, width, tag):
+            name = "h_words%d" % s0
+            h_words[s0] = sb.tile([P, width], U32, name=name, tag=tag or name, align_bytes=ALIGN)
+            nc.vector.quantize_mx(
+                out=h_words[s0][:].bitcast(FP8X4),
+                scales=h_scales[:, s0 : s0 + width],
+                in_=h_bf[:, PACK * s0 : PACK * (s0 + width)],
+            )
 
         def second_product(b, s0, width):
             cols = slice(s0, s0 + width)
-            res = psum.tile([P, width], F32, name="res%d" % s0, tag="bank%d" % b)
+            res = psum.tile([P, width], F32, name="res%d" % s0, tag="bank%d" % ((PACK + b) % (2 * PACK)))
             nc.tensor.matmul_mx(
                 out=res[:],
                 lhsT=w2_words[:].bitcast(FP8X4),
                 lhsT_scale=w2_scales[:],
-                rhs=h_words[:, cols].bitcast(FP8X4),
+                rhs=h_words[s0][:].bitcast(FP8X4),
                 rhs_scale=h_scales[:, cols],
                 start=True,
                 stop=True,
             )
-            staged = sb.tile([P, width], F32, name="staged%d" % s0, align_bytes=ALIGN)
-            nc.scalar.copy(out=staged[:], in_=res[:])
+            name = "staged%d" % s0
+            staged = sb.tile([P, width], F32, name=name, tag="pos768" if b == 0 else name, align_bytes=ALIGN)
+            if b in COPIES_ON_VECTOR:
+                nc.vector.tensor_copy(out=staged[:], in_=res[:])
+            else:
+                nc.scalar.copy(out=staged[:], in_=res[:])
             nc.sync.dma_start(out=out[:, cols], in_=staged[:])
 
         steps = spans(H_STEPS)
-        outs_by_end = {s0 + width: (b, s0, width) for b, (s0, width) in enumerate(spans(OUT_STEPS))}
-        for i in range(len(steps) + OUT_LAG):
-            if i < len(steps):
-                hidden(*steps[i])
-            if i == QUANTISE_LAG - 1:
-                nc.vector.quantize_mx(out=w2_words[:].bitcast(FP8X4), scales=w2_scales[:], in_=w2_bf[:])
-            if 0 <= i - QUANTISE_LAG < len(steps):
-                quantise_h(*steps[i - QUANTISE_LAG])
-            if i >= OUT_LAG and sum(steps[i - OUT_LAG]) in outs_by_end:
-                second_product(*outs_by_end[sum(steps[i - OUT_LAG])])
+        for i, step in enumerate(steps):
+            hidden(*step)
+            if sum(step) == PICKS[0]:
+                late_pieces()
+        nc.vector.quantize_mx(out=w2_words[:].bitcast(FP8X4), scales=w2_scales[:], in_=w2_bf[:])
+        for b, (s0, width) in enumerate(spans(OUT_STEPS)):
+            quantise_h(s0, width, H_WORDS_PLACES[b])
+            second_product(b, s0, width)

@@ -23,16 +23,20 @@ BANK = 512
 LIST_ROWS = 16
 ALIGN = 64
 
-X_PLAN = (
-    (((512, 3), (512, 3), (256, 4)), ((512, 5), (256, 5))),
-    (((512, 4), (512, 3)), ((512, 4),), ((256, 4),), ((256, 5),)),
-)
-X_LOADS = tuple(tuple(sum(width for width, share in load) for load in loads) for loads in X_PLAN)
-X_UNIT = 512
-W1_HALVES = 2
-W1_LAST_ON_VECTOR = 16
+PAIR = 2
+PAIRS = PACK // PAIR
+X_PLAN = {
+    (0, 0): ((2048, 11),),
+    (0, 1): ((1024, 0), (1024, 11)),
+    (1, 0): ((1024, 16), (1024, 5)),
+    (1, 1): ((768, 0), (768, 4), (512, 11)),
+}
+PICKS = ((512, 512), (256, 256, 256, 256))
+W1_ON_VECTOR = (48, 54)
+W1_QUANTISE = ((256, 256), (256, 256))
 POS_LOADS = (512, 256, 256)
-PICKS = (256, 256, 256, 256)
+OPEN_GROUPS = (256,)
+PROBES = ()
 H_STEPS = (128,) * 8
 OUT_STEPS = (256, 256, 256, 128, 128)
 H_WORDS_PLACES = ("pos0", "pre640", None, None, None)
@@ -58,29 +62,29 @@ def tile_picked_embpos_gelu_e_kernel(tc, xT, w1, w2, pos, offs, out):
         psum = ctx.enter_context(tc.psum_pool(name="psum", bufs=1))
 
         offsets = lists.tile([P, S // LIST_ROWS], U16, name="offsets")
-        x_scales = sb.tile([P, T], U8, name="x_scales", align_bytes=ALIGN)
-        nc.vector.memset(x_scales[:].bitcast(I32), 0)
         warm = sb.tile([P, 2], F32, name="warm")
         nc.gpsimd.memset(warm[:, 0:1], 0.0)
         nc.scalar.activation(warm[:, 1:2], warm[:, 0:1], GELU)
-        x_words = [sb.tile([P, T], U32, name="x_words%d" % g, align_bytes=ALIGN) for g in range(PASSES)]
+
+        w1_raw = {}
+
+        def load_w1(g):
+            rows = w1[g * K_PASS : (g + 1) * K_PASS, :].rearrange("(p j) c -> p j c", j=PACK)
+            name = "w1_raw%d" % g
+            w1_raw[g] = sb.tile([P, PACK, H], F32, name=name, tag=name, align_bytes=ALIGN)
+            nc.sync.dma_start(out=w1_raw[g][:], in_=rows)
 
         x_raw = {}
-        for g in range(PASSES):
-            rows = xT[g * K_PASS : (g + 1) * K_PASS, :].rearrange("(p j) c -> p j c", j=PACK)
-            for c0, width in spans(X_LOADS[g]):
-                x_raw[g, c0] = sb.tile([P, PACK, width], F32, name="x_raw%d_%d" % (g, c0), align_bytes=ALIGN)
-                nc.sync.dma_start(out=x_raw[g, c0][:], in_=rows[:, :, c0 : c0 + width])
-            if g == 0:
+        for (g, u), loads in X_PLAN.items():
+            rows = xT[g * K_PASS : (g + 1) * K_PASS, :].rearrange("(p u e) c -> p u e c", u=PAIRS, e=PAIR)
+            for c0, width in spans([width for width, share in loads]):
+                name = "x_raw%d_%d_%d" % (g, u, c0)
+                x_raw[g, u, c0] = sb.tile([P, PAIR, width], F32, name=name, tag=name, align_bytes=ALIGN)
+                nc.sync.dma_start(out=x_raw[g, u, c0][:], in_=rows[:, u, :, c0 : c0 + width])
+            if (g, u) == (0, 0):
                 nc.sync.dma_start(offsets[:], offs)
-        w1_raw = {}
-        channels = H // W1_HALVES
         for g in range(PASSES):
-            rows = w1[g * K_PASS : (g + 1) * K_PASS, :].rearrange("(p j) c -> p j c", j=PACK)
-            for a in range(W1_HALVES):
-                name = "w1_raw%d_%d" % (g, a)
-                w1_raw[g, a] = sb.tile([P, PACK, channels], F32, name=name, tag=name, align_bytes=ALIGN)
-                nc.sync.dma_start(out=w1_raw[g, a][:], in_=rows[:, :, a * channels : (a + 1) * channels])
+            load_w1(g)
         pos_rows = pos.rearrange("(p t) s -> p t s", t=PACK)
         pos_sb = {}
         w2_raw = sb.tile([P, PACK, N], F32, name="w2_raw", align_bytes=ALIGN)
@@ -90,33 +94,48 @@ def tile_picked_embpos_gelu_e_kernel(tc, xT, w1, w2, pos, offs, out):
             if s0 == 0:
                 nc.sync.dma_start(out=w2_raw[:], in_=w2.rearrange("(p j) n -> p j n", j=PACK))
 
-        def quantise_x(g, c0, width, eighths):
-            load0 = max(start for pass_of, start in x_raw if pass_of == g and start <= c0)
-            on_vector = width * eighths // 8
-            raw = x_raw[g, load0][:, :, c0 - load0 : c0 - load0 + width]
-            woven = sb.tile([P, width * PACK], BF16, name="x_bf%d_%d" % (g, c0), align_bytes=ALIGN)
-            dst, src = weave_views(woven[:, : on_vector * PACK], raw[:, :, :on_vector])
-            nc.vector.tensor_copy(out=dst, in_=src)
-            if on_vector < width:
-                dst, src = weave_views(woven[:, on_vector * PACK :], raw[:, :, on_vector:])
-                nc.scalar.copy(out=dst, in_=src)
-            cols = slice(c0, c0 + width)
-            nc.vector.quantize_mx(
-                out=x_words[g][:, cols].bitcast(FP8X4), scales=x_scales[PACK * g : P, cols], in_=woven[:]
+        def pair_window(g, u):
+            window = sb.tile([P, T], U32, name="x_pairs%d_%d" % (g, u), align_bytes=ALIGN)
+            loads = X_PLAN[g, u]
+            for (c0, width), (same, share) in zip(spans([width for width, share in loads]), loads):
+                split = width * share // 16
+                for engine_copy, a, b in ((nc.vector.tensor_copy, 0, split), (nc.scalar.copy, split, width)):
+                    if a < b:
+                        engine_copy(
+                            out=window[:, c0 + a : c0 + b].bitcast(BF16).rearrange("p (c e) -> p c e", e=PAIR),
+                            in_=x_raw[g, u, c0][:, :, a:b].rearrange("p e c -> p c e"),
+                        )
+            return window
+
+        picked = [sb.tile([P, PAIRS, S], U32, name="picked%d" % g, align_bytes=ALIGN) for g in range(PASSES)]
+        x_words = {(g, 0): sb.tile([P, S], U32, name="x_words%d" % g, align_bytes=ALIGN) for g in range(PASSES)}
+
+        def words_of(g, s0, width):
+            start = max(start for pass_of, start in x_words if pass_of == g and start <= s0)
+            return x_words[g, start][:, s0 - start : s0 - start + width].bitcast(FP8X4)
+        x_scales = [sb.tile([P, S], U8, name="x_scales%d" % g, align_bytes=ALIGN) for g in range(PASSES)]
+
+        def gather(window, g, u, s0, width):
+            entries = offsets[:, s0 // LIST_ROWS : (s0 + width) // LIST_ROWS]
+            nc.vector.tensor_copy(picked[g][:, u, s0 : s0 + width], window[:].indirect(entries))
+
+        x_bf = {}
+
+        def staging(entries, name, tag=None):
+            return sb.tile([P, entries * PAIRS], U32, name=name, tag=tag or name, align_bytes=ALIGN)
+
+        def weave_picked(g, s0, width, dst):
+            x_bf[g, s0] = dst
+            nc.scalar.copy(
+                out=dst.rearrange("p (s u) -> p s u", u=PAIRS),
+                in_=picked[g][:, :, s0 : s0 + width].rearrange("p u s -> p s u"),
             )
 
-        picks = spans(PICKS)
-        second_words = {}
-
-        def gather(window, s0, width, dtype, name, tag):
-            picked = sb.tile([P, width], dtype, name=name, tag=tag or name, align_bytes=ALIGN)
-            entries = offsets[:, s0 // LIST_ROWS : (s0 + width) // LIST_ROWS]
-            nc.vector.tensor_copy(picked[:], window[:].indirect(entries))
-            return picked
-
-        def gather_second_words(piece, tag=None):
-            second_words[piece] = gather(x_words[1], *picks[piece], U32, "picked_words1_%d" % piece, tag)
-
+        def quantise_picked(g, s0, width):
+            cols = slice(s0, s0 + width)
+            nc.vector.quantize_mx(
+                out=words_of(g, s0, width), scales=x_scales[g][:, cols], in_=x_bf[g, s0].bitcast(BF16)
+            )
 
         w1_bf = [
             sb.tile([P, PACK, P, PACK], BF16, name="w1_bf%d" % g, tag="w1_bf%d" % g, align_bytes=ALIGN)
@@ -125,35 +144,33 @@ def tile_picked_embpos_gelu_e_kernel(tc, xT, w1, w2, pos, offs, out):
         w1_words = [sb.tile([P, H], U32, name="w1_words%d" % g, align_bytes=ALIGN) for g in range(PASSES)]
         w1_scales = [sb.tile([P, H], U8, name="w1_scales%d" % g, align_bytes=ALIGN) for g in range(PASSES)]
 
-        def weave_w1(g, a):
-            ms = slice(a * (P // W1_HALVES), (a + 1) * (P // W1_HALVES))
-            dst = w1_bf[g][:, :, ms, :].rearrange("p t m j -> p m j t")
-            src = w1_raw[g, a][:].rearrange("p j (m t) -> p m j t", t=PACK)
-            split = W1_LAST_ON_VECTOR if (g, a) == (PASSES - 1, W1_HALVES - 1) else 0
+        def weave_w1(g):
+            dst = w1_bf[g][:].rearrange("p t m j -> p m j t")
+            src = w1_raw[g][:].rearrange("p j (m t) -> p m j t", t=PACK)
+            split = W1_ON_VECTOR[g]
             if split:
                 nc.vector.tensor_copy(out=dst[:, :split], in_=src[:, :split])
             nc.scalar.copy(out=dst[:, split:], in_=src[:, split:])
 
         def quantise_w1(g):
             flat = w1_bf[g][:].rearrange("p t m j -> p (t m j)")
-            for c0 in range(0, H, P):
-                cols = slice(c0, c0 + P)
+            for c0, width in spans(W1_QUANTISE[g]):
+                cols = slice(c0, c0 + width)
                 nc.vector.quantize_mx(
                     out=w1_words[g][:, cols].bitcast(FP8X4),
                     scales=w1_scales[g][:, cols],
-                    in_=flat[:, PACK * c0 : PACK * (c0 + P)],
+                    in_=flat[:, PACK * c0 : PACK * (c0 + width)],
                 )
 
-        def first_product_pass(acc_ap, g, t, piece, s0, width):
+        def first_product_pass(acc_ap, g, t, s0, width):
             cols = slice(t * P, (t + 1) * P)
-            in_piece = slice(s0 - picks[piece][0], s0 - picks[piece][0] + width)
-            words = first_words[:, s0 : s0 + width] if g == 0 else second_words[piece][:, in_piece]
+            entries = slice(s0, s0 + width)
             nc.tensor.matmul_mx(
                 out=acc_ap,
                 lhsT=w1_words[g][:, cols].bitcast(FP8X4),
                 lhsT_scale=w1_scales[g][:, cols],
-                rhs=words.bitcast(FP8X4),
-                rhs_scale=picked_scales[s0 // (S // 2)][PACK * g : P, s0 % (S // 2) : s0 % (S // 2) + width],
+                rhs=words_of(g, s0, width),
+                rhs_scale=x_scales[g][:, entries],
                 start=(g == 0),
                 stop=(g == PASSES - 1),
             )
@@ -164,45 +181,53 @@ def tile_picked_embpos_gelu_e_kernel(tc, xT, w1, w2, pos, offs, out):
                 for b in range(first_bank, first_bank + PACK // per_bank)
             ]
 
-        def quantise_pass(g):
-            units = [unit for load in X_PLAN[g] for unit in load]
-            for (c0, width), (same, eighths) in zip(spans([width for width, eighths in units]), units):
-                quantise_x(g, c0, width, eighths)
+        def probe(name, ap):
+            if name in PROBES:
+                mark = sb.tile([P, 1], ap.dtype, name="probe_" + name)
+                nc.gpsimd.tensor_copy(mark[:], ap)
 
-        quantise_pass(0)
-        first_words = sb.tile([P, S], U32, name="picked_words0", align_bytes=ALIGN)
-        nc.vector.tensor_copy(first_words[:], x_words[0][:].indirect(offsets[:]))
-        quantise_pass(1)
+        groups = spans(OPEN_GROUPS)
+        acc = {s0: banks_for(PACK * b, width, 1) for b, (s0, width) in enumerate(groups)}
 
-        picked_scales = {0: gather(x_scales, 0, S // 2, U8, "picked_scales0", None)}
-        gather_second_words(0)
-        gather_second_words(1)
-        weave_w1(0, 0)
-        weave_w1(0, 1)
-        quantise_w1(0)
-        acc = {picks[0][0]: banks_for(0, PICKS[0], 1), picks[1][0]: banks_for(PACK, PICKS[1], 1)}
+        def open_pass(g, s0, width):
+            for t in range(PACK):
+                first_product_pass(acc[s0][t][:, 0, :], g, t, s0, width)
 
-        def open_pieces_pass(g):
-            for piece in range(2):
-                s0, width = picks[piece]
-                for t in range(PACK):
-                    first_product_pass(acc[s0][t][:, 0, :], g, t, piece, s0, width)
+        for g in range(PASSES):
+            pieces = spans(PICKS[g])
+            window = pair_window(g, 0)
+            gather(window, g, 0, 0, S)
+            probe("g%d0" % g, picked[g][:, 0, 0:1])
+            window = pair_window(g, 1)
+            for s0, width in pieces:
+                gather(window, g, 1, s0, width)
+            for s0, width in pieces[:2]:
+                weave_picked(g, s0, width, staging(width, "x_bf%d_%d" % (g, s0))[:])
+                quantise_picked(g, s0, width)
+            probe("g%d1" % g, picked[g][:, 1, S - 1 : S])
+        for g in range(PASSES):
+            weave_w1(g)
+            quantise_w1(g)
+            probe("w1q%d" % g, w1_words[g][:, H - 1 : H])
+            for group in groups:
+                open_pass(g, *group)
+        late = staging(S // 2, "x_bf1_late", "w1_raw1")
+        x_words[1, S // 2] = sb.tile([P, S // 2], U32, name="x_words1_late", tag="w1_bf1", align_bytes=ALIGN)
+        for s0, width in spans(PICKS[1])[2:]:
+            weave_picked(1, s0, width, late[:, PAIRS * (s0 - S // 2) : PAIRS * (s0 - S // 2 + width)])
+            quantise_picked(1, s0, width)
 
-        open_pieces_pass(0)
-        picked_scales[1] = gather(x_scales, S // 2, S // 2, U8, "picked_scales1", "w1_bf0")
-        weave_w1(1, 0)
-        gather_second_words(2, tag="w1_raw1_0")
-        weave_w1(1, 1)
-        quantise_w1(1)
-        open_pieces_pass(1)
-        gather_second_words(3, tag="w1_bf1")
-
-        def late_pieces():
-            for b, s0 in enumerate(range(picks[2][0], S, P)):
-                acc[s0] = banks_for(b, P, PACK)
+        def closed_groups(first_bank, start, stop):
+            for b, s0 in enumerate(range(start, stop, P)):
+                acc[s0] = banks_for(first_bank + b, P, PACK)
                 for t in range(PACK):
                     for g in range(PASSES):
-                        first_product_pass(acc[s0][0][:, t, :], g, t, 2 + b // 2, s0, P)
+                        first_product_pass(acc[s0][0][:, t, :], g, t, s0, P)
+
+        closed_groups(PACK, OPEN_GROUPS[0], OPEN_GROUPS[0] + PACK * P)
+
+        def late_pieces():
+            closed_groups(0, OPEN_GROUPS[0] + PACK * P, S)
 
         w2_bf = sb.tile([P, N * PACK], BF16, name="w2_bf", align_bytes=ALIGN)
         w2_words = sb.tile([P, N], U32, name="w2_words", align_bytes=ALIGN)
@@ -229,6 +254,7 @@ def tile_picked_embpos_gelu_e_kernel(tc, xT, w1, w2, pos, offs, out):
                 )
             dst, src = weave_views(h_bf[:, PACK * s0 : PACK * (s0 + width)], pre[:])
             nc.scalar.activation(dst, src, GELU)
+            probe("gelu%d" % s0, h_bf[:, PACK * s0 : PACK * s0 + 1])
 
         def quantise_h(s0, width, tag):
             name = "h_words%d" % s0
@@ -241,7 +267,7 @@ def tile_picked_embpos_gelu_e_kernel(tc, xT, w1, w2, pos, offs, out):
 
         def second_product(b, s0, width):
             cols = slice(s0, s0 + width)
-            res = psum.tile([P, width], F32, name="res%d" % s0, tag="bank%d" % ((PACK + b) % (2 * PACK)))
+            res = psum.tile([P, width], F32, name="res%d" % s0, tag="bank%d" % (2 + b))
             nc.tensor.matmul_mx(
                 out=res[:],
                 lhsT=w2_words[:].bitcast(FP8X4),
@@ -262,7 +288,7 @@ def tile_picked_embpos_gelu_e_kernel(tc, xT, w1, w2, pos, offs, out):
         steps = spans(H_STEPS)
         for i, step in enumerate(steps):
             hidden(*step)
-            if sum(step) == PICKS[0]:
+            if sum(step) == OPEN_GROUPS[0]:
                 late_pieces()
         nc.vector.quantize_mx(out=w2_words[:].bitcast(FP8X4), scales=w2_scales[:], in_=w2_bf[:])
         for b, (s0, width) in enumerate(spans(OUT_STEPS)):

@@ -7,40 +7,42 @@ FLOPS = 2 * S * (K * H + H * N)
 
 F32 = mybir.dt.float32
 BF16 = mybir.dt.bfloat16
-I32 = mybir.dt.int32
 U32 = mybir.dt.uint32
 U16 = mybir.dt.uint16
 U8 = mybir.dt.uint8
 FP8X4 = mybir.dt.float8_e4m3fn_x4
 GELU = mybir.ActivationFunctionType.Gelu_apprx_tanh
+COPY = mybir.ActivationFunctionType.Copy
 ADD = mybir.AluOpType.add
 
 P = 128
 PACK = 4
 K_PASS = P * PACK
 PASSES = K // K_PASS
-BANK = 512
 LIST_ROWS = 16
 ALIGN = 64
 
-PAIR = 2
-PAIRS = PACK // PAIR
-X_PLAN = {
-    (0, 0): ((2048, 11),),
-    (0, 1): ((1024, 0), (1024, 11)),
-    (1, 0): ((1024, 16), (1024, 5)),
-    (1, 1): ((768, 0), (768, 4), (512, 11)),
+GATHERS = {
+    (0, 0): (("vector", 512), ("scalar", 512)),
+    (0, 1): (("vector", 512), ("scalar", 512)),
+    (0, 2): (("vector", 512), ("scalar", 512)),
+    (0, 3): (("vector", 512), ("scalar", 512)),
+    (1, 0): (("vector", 128), ("scalar", 896)),
+    (1, 1): (("vector", 384), ("scalar", 640)),
+    (1, 2): (("vector", 512), ("scalar", 512)),
+    (1, 3): (("vector", 256), ("scalar", 768)),
 }
-PICKS = ((512, 512), (256, 256, 256, 256))
-W1_ON_VECTOR = (48, 54)
-W1_QUANTISE = ((256, 256), (256, 256))
-POS_LOADS = (512, 256, 256)
-OPEN_GROUPS = (256,)
-PROBES = ()
-H_STEPS = (128,) * 8
+X_QUANTISE = (512, 512)
+LAST_PIECES = (256, 512, 256)
+
+W1_ON_VECTOR = (128, 80)
+W1_QUANTISE = ((512,), (512,))
+POS_LOADS = (384, 384, 256)
+STEP = 128
+OPEN_BANKS = 2
 OUT_STEPS = (256, 256, 256, 128, 128)
-H_WORDS_PLACES = ("pos0", "pre640", None, None, None)
-COPIES_ON_VECTOR = (0, 3)
+COPIES_ON_VECTOR = (2, 3)
+PROBES = ()
 
 
 def spans(widths):
@@ -61,96 +63,93 @@ def tile_picked_embpos_gelu_e_kernel(tc, xT, w1, w2, pos, offs, out):
         sb = ctx.enter_context(tc.tile_pool(name="sb", bufs=1))
         psum = ctx.enter_context(tc.psum_pool(name="psum", bufs=1))
 
+        def sbuf(shape, dtype, name, tag=None):
+            return sb.tile(shape, dtype, name=name, tag=tag or name, align_bytes=ALIGN)
+
+        def probe(name, ap):
+            if name in PROBES:
+                mark = sbuf([P, 1], ap.dtype, "probe_" + name)
+                nc.gpsimd.tensor_copy(mark[:], ap)
+
         offsets = lists.tile([P, S // LIST_ROWS], U16, name="offsets")
-        warm = sb.tile([P, 2], F32, name="warm")
+        warm = sbuf([P, 2], F32, "warm")
         nc.gpsimd.memset(warm[:, 0:1], 0.0)
         nc.scalar.activation(warm[:, 1:2], warm[:, 0:1], GELU)
 
-        w1_raw = {}
-
-        def load_w1(g):
-            rows = w1[g * K_PASS : (g + 1) * K_PASS, :].rearrange("(p j) c -> p j c", j=PACK)
-            name = "w1_raw%d" % g
-            w1_raw[g] = sb.tile([P, PACK, H], F32, name=name, tag=name, align_bytes=ALIGN)
-            nc.sync.dma_start(out=w1_raw[g][:], in_=rows)
-
-        x_raw = {}
-        for (g, u), loads in X_PLAN.items():
-            rows = xT[g * K_PASS : (g + 1) * K_PASS, :].rearrange("(p u e) c -> p u e c", u=PAIRS, e=PAIR)
-            for c0, width in spans([width for width, share in loads]):
-                name = "x_raw%d_%d_%d" % (g, u, c0)
-                x_raw[g, u, c0] = sb.tile([P, PAIR, width], F32, name=name, tag=name, align_bytes=ALIGN)
-                nc.sync.dma_start(out=x_raw[g, u, c0][:], in_=rows[:, u, :, c0 : c0 + width])
-            if (g, u) == (0, 0):
-                nc.sync.dma_start(offsets[:], offs)
+        planes = {}
+        x_rows = xT.rearrange("(g p j) c -> g j p c", g=PASSES, j=PACK)
         for g in range(PASSES):
-            load_w1(g)
+            for j in range(PACK):
+                planes[g, j] = sbuf([P, T], F32, "plane%d_%d" % (g, j))
+                nc.sync.dma_start(out=planes[g, j][:], in_=x_rows[g, j])
+                if (g, j) == (0, 0):
+                    nc.sync.dma_start(offsets[:], offs)
+        w1_raw = []
+        for g in range(PASSES):
+            w1_raw.append(sbuf([P, PACK, H], F32, "w1_raw%d" % g))
+            rows = w1[g * K_PASS : (g + 1) * K_PASS, :].rearrange("(p j) c -> p j c", j=PACK)
+            nc.sync.dma_start(out=w1_raw[g][:], in_=rows)
         pos_rows = pos.rearrange("(p t) s -> p t s", t=PACK)
         pos_sb = {}
-        w2_raw = sb.tile([P, PACK, N], F32, name="w2_raw", align_bytes=ALIGN)
+        w2_raw = sbuf([P, PACK, N], F32, "w2_raw")
+        nc.sync.dma_start(out=w2_raw[:], in_=w2.rearrange("(p j) n -> p j n", j=PACK))
         for s0, width in spans(POS_LOADS):
-            pos_sb[s0] = sb.tile([P, PACK, width], F32, name="pos%d" % s0, tag="pos%d" % s0, align_bytes=ALIGN)
+            pos_sb[s0] = sbuf([P, PACK, width], F32, "pos%d" % s0)
             nc.sync.dma_start(out=pos_sb[s0][:], in_=pos_rows[:, :, s0 : s0 + width])
-            if s0 == 0:
-                nc.sync.dma_start(out=w2_raw[:], in_=w2.rearrange("(p j) n -> p j n", j=PACK))
 
-        def pair_window(g, u):
-            window = sb.tile([P, T], U32, name="x_pairs%d_%d" % (g, u), align_bytes=ALIGN)
-            loads = X_PLAN[g, u]
-            for (c0, width), (same, share) in zip(spans([width for width, share in loads]), loads):
-                split = width * share // 16
-                for engine_copy, a, b in ((nc.vector.tensor_copy, 0, split), (nc.scalar.copy, split, width)):
-                    if a < b:
-                        engine_copy(
-                            out=window[:, c0 + a : c0 + b].bitcast(BF16).rearrange("p (c e) -> p c e", e=PAIR),
-                            in_=x_raw[g, u, c0][:, :, a:b].rearrange("p e c -> p c e"),
-                        )
-            return window
-
-        picked = [sb.tile([P, PAIRS, S], U32, name="picked%d" % g, align_bytes=ALIGN) for g in range(PASSES)]
-        x_words = {(g, 0): sb.tile([P, S], U32, name="x_words%d" % g, align_bytes=ALIGN) for g in range(PASSES)}
-
-        def words_of(g, s0, width):
-            start = max(start for pass_of, start in x_words if pass_of == g and start <= s0)
-            return x_words[g, start][:, s0 - start : s0 - start + width].bitcast(FP8X4)
-        x_scales = [sb.tile([P, S], U8, name="x_scales%d" % g, align_bytes=ALIGN) for g in range(PASSES)]
-
-        def gather(window, g, u, s0, width):
-            entries = offsets[:, s0 // LIST_ROWS : (s0 + width) // LIST_ROWS]
-            nc.vector.tensor_copy(picked[g][:, u, s0 : s0 + width], window[:].indirect(entries))
-
+        picked = [sbuf([P, PACK, S], F32, "picked%d" % g) for g in range(PASSES)]
         x_bf = {}
+        x_words = {}
+        x_scales = [sbuf([P, S], U8, "x_scales%d" % g) for g in range(PASSES)]
 
-        def staging(entries, name, tag=None):
-            return sb.tile([P, entries * PAIRS], U32, name=name, tag=tag or name, align_bytes=ALIGN)
+        def gather_plane(g, j, pieces):
+            for (s0, width), (engine, same) in zip(spans([width for engine, width in pieces]), pieces):
+                looked_up = planes[g, j][:].indirect(offsets[:, s0 // LIST_ROWS : (s0 + width) // LIST_ROWS])
+                if engine == "vector":
+                    nc.vector.tensor_copy(picked[g][:, j, s0 : s0 + width], looked_up)
+                else:
+                    nc.scalar.activation(picked[g][:, j, s0 : s0 + width], looked_up, COPY)
 
-        def weave_picked(g, s0, width, dst):
-            x_bf[g, s0] = dst
-            nc.scalar.copy(
-                out=dst.rearrange("p (s u) -> p s u", u=PAIRS),
-                in_=picked[g][:, :, s0 : s0 + width].rearrange("p u s -> p s u"),
-            )
+        def weave_x(g, s0, width, on_scalar=0, tag=None):
+            x_bf[g, s0] = sbuf([P, PACK * width], BF16, "x_bf%d_%d" % (g, s0), tag)
+            for copy, a, b in ((nc.scalar.copy, 0, on_scalar), (nc.vector.tensor_copy, on_scalar, width)):
+                if a < b:
+                    dst, src = weave_views(x_bf[g, s0][:, PACK * a : PACK * b], picked[g][:, :, s0 + a : s0 + b])
+                    copy(out=dst, in_=src)
 
-        def quantise_picked(g, s0, width):
-            cols = slice(s0, s0 + width)
+        def quantise_x(g, s0, width, tag=None):
+            x_words[g, s0] = sbuf([P, width], U32, "x_words%d_%d" % (g, s0), tag)
             nc.vector.quantize_mx(
-                out=words_of(g, s0, width), scales=x_scales[g][:, cols], in_=x_bf[g, s0].bitcast(BF16)
+                out=x_words[g, s0][:].bitcast(FP8X4),
+                scales=x_scales[g][:, s0 : s0 + width],
+                in_=x_bf[g, s0][:],
             )
 
-        w1_bf = [
-            sb.tile([P, PACK, P, PACK], BF16, name="w1_bf%d" % g, tag="w1_bf%d" % g, align_bytes=ALIGN)
-            for g in range(PASSES)
-        ]
-        w1_words = [sb.tile([P, H], U32, name="w1_words%d" % g, align_bytes=ALIGN) for g in range(PASSES)]
-        w1_scales = [sb.tile([P, H], U8, name="w1_scales%d" % g, align_bytes=ALIGN) for g in range(PASSES)]
+        for g in range(PASSES):
+            for j in range(PACK):
+                gather_plane(g, j, GATHERS[g, j])
+                probe("g%d%d" % (g, j), picked[g][:, j, S - 1 : S])
+            if g == 0:
+                for piece in spans(X_QUANTISE):
+                    weave_x(g, *piece)
+                for piece in spans(X_QUANTISE):
+                    quantise_x(g, *piece)
+        first, second, late = spans(LAST_PIECES)
+        weave_x(1, *first)
+        quantise_x(1, *first)
+        weave_x(1, *second, on_scalar=second[1])
+
+        w1_bf = [sbuf([P, PACK, P, PACK], BF16, "w1_bf%d" % g) for g in range(PASSES)]
+        w1_words = [sbuf([P, H], U32, "w1_words%d" % g) for g in range(PASSES)]
+        w1_scales = [sbuf([P, H], U8, "w1_scales%d" % g) for g in range(PASSES)]
 
         def weave_w1(g):
             dst = w1_bf[g][:].rearrange("p t m j -> p m j t")
             src = w1_raw[g][:].rearrange("p j (m t) -> p m j t", t=PACK)
             split = W1_ON_VECTOR[g]
-            if split:
-                nc.vector.tensor_copy(out=dst[:, :split], in_=src[:, :split])
-            nc.scalar.copy(out=dst[:, split:], in_=src[:, split:])
+            nc.vector.tensor_copy(out=dst[:, :split], in_=src[:, :split])
+            if split < P:
+                nc.scalar.copy(out=dst[:, split:], in_=src[:, split:])
 
         def quantise_w1(g):
             flat = w1_bf[g][:].rearrange("p t m j -> p (t m j)")
@@ -162,135 +161,83 @@ def tile_picked_embpos_gelu_e_kernel(tc, xT, w1, w2, pos, offs, out):
                     in_=flat[:, PACK * c0 : PACK * (c0 + width)],
                 )
 
-        def first_product_pass(acc_ap, g, t, s0, width):
+        steps = S // STEP
+        acc = [psum.tile([P, PACK, STEP], F32, name="acc%d" % b, tag="bank%d" % b) for b in range(steps)]
+
+        def first_product_pass(b, g, t, start, stop):
             cols = slice(t * P, (t + 1) * P)
-            entries = slice(s0, s0 + width)
+            entries = slice(b * STEP, (b + 1) * STEP)
+            piece = max(s0 for s0, width in spans((X_QUANTISE, LAST_PIECES)[g]) if s0 <= b * STEP)
             nc.tensor.matmul_mx(
-                out=acc_ap,
+                out=acc[b][:, t, :],
                 lhsT=w1_words[g][:, cols].bitcast(FP8X4),
                 lhsT_scale=w1_scales[g][:, cols],
-                rhs=words_of(g, s0, width),
+                rhs=x_words[g, piece][:, b * STEP - piece : (b + 1) * STEP - piece].bitcast(FP8X4),
                 rhs_scale=x_scales[g][:, entries],
-                start=(g == 0),
-                stop=(g == PASSES - 1),
+                start=start,
+                stop=stop,
             )
 
-        def banks_for(first_bank, width, per_bank):
-            return [
-                psum.tile([P, per_bank, width], F32, name="acc%d" % b, tag="bank%d" % b)
-                for b in range(first_bank, first_bank + PACK // per_bank)
-            ]
-
-        def probe(name, ap):
-            if name in PROBES:
-                mark = sb.tile([P, 1], ap.dtype, name="probe_" + name)
-                nc.gpsimd.tensor_copy(mark[:], ap)
-
-        groups = spans(OPEN_GROUPS)
-        acc = {s0: banks_for(PACK * b, width, 1) for b, (s0, width) in enumerate(groups)}
-
-        def open_pass(g, s0, width):
-            for t in range(PACK):
-                first_product_pass(acc[s0][t][:, 0, :], g, t, s0, width)
-
-        for g in range(PASSES):
-            pieces = spans(PICKS[g])
-            window = pair_window(g, 0)
-            gather(window, g, 0, 0, S)
-            probe("g%d0" % g, picked[g][:, 0, 0:1])
-            window = pair_window(g, 1)
-            for s0, width in pieces:
-                gather(window, g, 1, s0, width)
-            for s0, width in pieces[:2]:
-                weave_picked(g, s0, width, staging(width, "x_bf%d_%d" % (g, s0))[:])
-                quantise_picked(g, s0, width)
-            probe("g%d1" % g, picked[g][:, 1, S - 1 : S])
         for g in range(PASSES):
             weave_w1(g)
             quantise_w1(g)
             probe("w1q%d" % g, w1_words[g][:, H - 1 : H])
-            for group in groups:
-                open_pass(g, *group)
-        late = staging(S // 2, "x_bf1_late", "w1_raw1")
-        x_words[1, S // 2] = sb.tile([P, S // 2], U32, name="x_words1_late", tag="w1_bf1", align_bytes=ALIGN)
-        for s0, width in spans(PICKS[1])[2:]:
-            weave_picked(1, s0, width, late[:, PAIRS * (s0 - S // 2) : PAIRS * (s0 - S // 2 + width)])
-            quantise_picked(1, s0, width)
-
-        def closed_groups(first_bank, start, stop):
-            for b, s0 in enumerate(range(start, stop, P)):
-                acc[s0] = banks_for(first_bank + b, P, PACK)
+            for b in range(OPEN_BANKS):
                 for t in range(PACK):
-                    for g in range(PASSES):
-                        first_product_pass(acc[s0][0][:, t, :], g, t, s0, P)
+                    first_product_pass(b, g, t, (g, t) == (0, 0), (g, t) == (PASSES - 1, PACK - 1))
+        quantise_x(1, *second, tag="w1_bf1")
+        weave_x(1, *late, on_scalar=late[1], tag="w1_raw1")
+        quantise_x(1, *late)
+        for b in range(OPEN_BANKS, steps):
+            for t in range(PACK):
+                for g in reversed(range(PASSES)):
+                    first_product_pass(b, g, t, g == PASSES - 1, g == 0)
 
-        closed_groups(PACK, OPEN_GROUPS[0], OPEN_GROUPS[0] + PACK * P)
+        w2_bf = sbuf([P, N * PACK], BF16, "w2_bf")
+        w2_words = sbuf([P, N], U32, "w2_words")
+        w2_scales = sbuf([P, N], U8, "w2_scales")
+        h_bf = sbuf([P, S * PACK], BF16, "h_bf")
+        h_words = sbuf([P, S], U32, "h_words")
+        h_scales = sbuf([P, S], U8, "h_scales")
 
-        def late_pieces():
-            closed_groups(0, OPEN_GROUPS[0] + PACK * P, S)
-
-        w2_bf = sb.tile([P, N * PACK], BF16, name="w2_bf", align_bytes=ALIGN)
-        w2_words = sb.tile([P, N], U32, name="w2_words", align_bytes=ALIGN)
-        w2_scales = sb.tile([P, N], U8, name="w2_scales", align_bytes=ALIGN)
-        dst, src = weave_views(w2_bf[:], w2_raw[:])
-        nc.scalar.copy(out=dst, in_=src)
-
-        h_bf = sb.tile([P, S * PACK], BF16, name="h_bf", align_bytes=ALIGN)
-        h_words = {}
-        h_scales = sb.tile([P, S], U8, name="h_scales", align_bytes=ALIGN)
-
-        def hidden(s0, width):
-            acc0 = max(start for start in acc if start <= s0)
+        def hidden(b):
+            s0 = b * STEP
             pos0 = max(start for start in pos_sb if start <= s0)
-            pre = sb.tile([P, PACK, width], F32, name="pre%d" % s0, tag="pre%d" % s0, align_bytes=ALIGN)
-            per_bank = PACK // len(acc[acc0])
-            for b, bank in enumerate(acc[acc0]):
-                ts = slice(b * per_bank, (b + 1) * per_bank)
-                nc.vector.tensor_tensor(
-                    pre[:, ts, :],
-                    bank[:, :, s0 - acc0 : s0 - acc0 + width],
-                    pos_sb[pos0][:, ts, s0 - pos0 : s0 - pos0 + width],
-                    ADD,
-                )
-            dst, src = weave_views(h_bf[:, PACK * s0 : PACK * (s0 + width)], pre[:])
+            pre = sbuf([P, PACK, STEP], F32, "pre%d" % b)
+            nc.vector.tensor_tensor(pre[:], acc[b][:], pos_sb[pos0][:, :, s0 - pos0 : s0 - pos0 + STEP], ADD)
+            probe("add%d" % b, pre[:, 0, 0:1])
+            dst, src = weave_views(h_bf[:, PACK * s0 : PACK * (s0 + STEP)], pre[:])
             nc.scalar.activation(dst, src, GELU)
-            probe("gelu%d" % s0, h_bf[:, PACK * s0 : PACK * s0 + 1])
-
-        def quantise_h(s0, width, tag):
-            name = "h_words%d" % s0
-            h_words[s0] = sb.tile([P, width], U32, name=name, tag=tag or name, align_bytes=ALIGN)
-            nc.vector.quantize_mx(
-                out=h_words[s0][:].bitcast(FP8X4),
-                scales=h_scales[:, s0 : s0 + width],
-                in_=h_bf[:, PACK * s0 : PACK * (s0 + width)],
-            )
+            probe("gelu%d" % b, h_bf[:, PACK * s0 : PACK * s0 + 1])
 
         def second_product(b, s0, width):
             cols = slice(s0, s0 + width)
-            res = psum.tile([P, width], F32, name="res%d" % s0, tag="bank%d" % (2 + b))
+            nc.vector.quantize_mx(
+                out=h_words[:, cols].bitcast(FP8X4),
+                scales=h_scales[:, cols],
+                in_=h_bf[:, PACK * s0 : PACK * (s0 + width)],
+            )
+            res = psum.tile([P, width], F32, name="res%d" % b, tag="bank%d" % b)
             nc.tensor.matmul_mx(
                 out=res[:],
                 lhsT=w2_words[:].bitcast(FP8X4),
                 lhsT_scale=w2_scales[:],
-                rhs=h_words[s0][:].bitcast(FP8X4),
+                rhs=h_words[:, cols].bitcast(FP8X4),
                 rhs_scale=h_scales[:, cols],
                 start=True,
                 stop=True,
             )
-            name = "staged%d" % s0
-            staged = sb.tile([P, width], F32, name=name, tag="pos768" if b == 0 else name, align_bytes=ALIGN)
+            staged = sbuf([P, width], F32, "staged%d" % b)
             if b in COPIES_ON_VECTOR:
                 nc.vector.tensor_copy(out=staged[:], in_=res[:])
             else:
                 nc.scalar.copy(out=staged[:], in_=res[:])
             nc.sync.dma_start(out=out[:, cols], in_=staged[:])
 
-        steps = spans(H_STEPS)
-        for i, step in enumerate(steps):
-            hidden(*step)
-            if sum(step) == OPEN_GROUPS[0]:
-                late_pieces()
+        for b in range(steps):
+            hidden(b)
+        dst, src = weave_views(w2_bf[:], w2_raw[:])
+        nc.scalar.copy(out=dst, in_=src)
         nc.vector.quantize_mx(out=w2_words[:].bitcast(FP8X4), scales=w2_scales[:], in_=w2_bf[:])
         for b, (s0, width) in enumerate(spans(OUT_STEPS)):
-            quantise_h(s0, width, H_WORDS_PLACES[b])
             second_product(b, s0, width)

@@ -23,13 +23,13 @@ LIST_ROWS = 16
 ALIGN = 64
 
 GATHERS = {
-    (0, 0): (("vector", 512), ("scalar", 512)),
-    (0, 1): (("vector", 512), ("scalar", 512)),
-    (0, 2): (("vector", 512), ("scalar", 512)),
-    (0, 3): (("vector", 512), ("scalar", 512)),
-    (1, 0): (("vector", 128), ("scalar", 896)),
-    (1, 1): (("vector", 384), ("scalar", 640)),
-    (1, 2): (("vector", 512), ("scalar", 512)),
+    (0, 0): (("scalar", 1024),),
+    (0, 1): (("vector", 1024),),
+    (0, 2): (("scalar", 1024),),
+    (0, 3): (("vector", 1024),),
+    (1, 0): (("scalar", 1024),),
+    (1, 1): (("vector", 256), ("scalar", 768)),
+    (1, 2): (("vector", 416), ("scalar", 608)),
     (1, 3): (("vector", 256), ("scalar", 768)),
 }
 X_QUANTISE = (512, 512)
@@ -80,8 +80,16 @@ def tile_picked_embpos_gelu_e_kernel(tc, xT, w1, w2, pos, offs, out):
         x_rows = xT.rearrange("(g p j) c -> g j p c", g=PASSES, j=PACK)
         for g in range(PASSES):
             for j in range(PACK):
-                planes[g, j] = sbuf([P, T], F32, "plane%d_%d" % (g, j))
-                nc.sync.dma_start(out=planes[g, j][:], in_=x_rows[g, j])
+                if g == 0 and j % 2 == 0:
+                    pair = sbuf([P, 2 * T], F32, "pair%d" % j)
+                    rows = xT[:K_PASS, :].rearrange("(p u e) c -> u p (e c)", u=2, e=2)
+                    nc.sync.dma_start(out=pair[:], in_=rows[j // 2])
+                    planes[g, j] = pair[:]
+                    planes[g, j + 1] = pair[:, T:]
+                elif g > 0:
+                    plane = sbuf([P, T], F32, "plane%d_%d" % (g, j))
+                    nc.sync.dma_start(out=plane[:], in_=x_rows[g, j])
+                    planes[g, j] = plane[:]
                 if (g, j) == (0, 0):
                     nc.sync.dma_start(offsets[:], offs)
         w1_raw = []
@@ -104,7 +112,7 @@ def tile_picked_embpos_gelu_e_kernel(tc, xT, w1, w2, pos, offs, out):
 
         def gather_plane(g, j, pieces):
             for (s0, width), (engine, same) in zip(spans([width for engine, width in pieces]), pieces):
-                looked_up = planes[g, j][:].indirect(offsets[:, s0 // LIST_ROWS : (s0 + width) // LIST_ROWS])
+                looked_up = planes[g, j].indirect(offsets[:, s0 // LIST_ROWS : (s0 + width) // LIST_ROWS])
                 if engine == "vector":
                     nc.vector.tensor_copy(picked[g][:, j, s0 : s0 + width], looked_up)
                 else:

@@ -21,27 +21,41 @@ K_PASS = P * PACK
 PASSES = K // K_PASS
 LIST_ROWS = 16
 ALIGN = 64
+BANK = 512
+WALK = 4
 
+X_LOADS = ((0, 0, 2), (0, 2, 2), (1, 0, 2), (1, 2, 1), (1, 3, 1))
+PLANE_5 = (("vector", 1024),)
+PLANE_6 = (("vector", 256), ("scalar", 768))
+LAST_PLANE = (("vector", 128), ("vector", 256), ("scalar", 128), ("scalar", 512))
 GATHERS = {
     (0, 0): (("scalar", 1024),),
     (0, 1): (("vector", 1024),),
     (0, 2): (("scalar", 1024),),
     (0, 3): (("vector", 1024),),
     (1, 0): (("scalar", 1024),),
-    (1, 1): (("vector", 256), ("scalar", 768)),
-    (1, 2): (("vector", 416), ("scalar", 608)),
-    (1, 3): (("vector", 256), ("scalar", 768)),
+    (1, 1): PLANE_5,
+    (1, 2): PLANE_6,
+    (1, 3): LAST_PLANE,
 }
-X_QUANTISE = (512, 512)
-LAST_PIECES = (256, 512, 256)
-
+X_BEHIND_W1 = 0
+PICKED_TILES = ((1024,), (1024,))
+W1_BYTES = 8192
+W1_TILES = ((2, 2), (2, 2))
+W1_QUANTISE = ((2, 2), (2, 1, 1))
+POS_BYTES = 2 * W1_BYTES
+PRE_BYTES = 4 * W1_BYTES
+COPY_BEHIND_GELU = 6
+X_PIECES = ((512, 128, 384), (128, 128, 256, 256, 128, 128))
+W1_LOADS = ((0, 0, 128), (1, 0, 128))
 W1_ON_VECTOR = (128, 80)
-W1_QUANTISE = ((512,), (512,))
-POS_LOADS = (384, 384, 256)
-STEP = 128
-OPEN_BANKS = 2
+POS_LOADS = (256, 256, 256, 128, 128)
+STEPS = (128, 128, 128, 128, 128, 128, 128, 128)
+POS_AHEAD_OF_W2 = 0
+STORES = (256, 256, 256, 128, 128)
+H_BEHIND = 512
+OPEN_STEPS = 3
 OUT_STEPS = (256, 256, 256, 128, 128)
-COPIES_ON_VECTOR = (2, 3)
 PROBES = ()
 
 
@@ -51,8 +65,8 @@ def spans(widths):
 
 def weave_views(dst, src):
     return (
-        dst.rearrange("p (c i j) -> p c j i", i=4, j=PACK),
-        src.rearrange("p j (c i) -> p c j i", i=4),
+        dst.rearrange("p (c i j) -> p c j i", i=WALK, j=PACK),
+        src.rearrange("p j (c i) -> p c j i", i=WALK),
     )
 
 
@@ -63,7 +77,11 @@ def tile_picked_embpos_gelu_e_kernel(tc, xT, w1, w2, pos, offs, out):
         sb = ctx.enter_context(tc.tile_pool(name="sb", bufs=1))
         psum = ctx.enter_context(tc.psum_pool(name="psum", bufs=1))
 
+        shared = ctx.enter_context(tc.tile_pool(name="shared", bufs=1))
+
         def sbuf(shape, dtype, name, tag=None):
+            if isinstance(tag, int):
+                return shared.tile(shape, dtype, name=name, tag=name, align_bytes=ALIGN, offset=tag)
             return sb.tile(shape, dtype, name=name, tag=tag or name, align_bytes=ALIGN)
 
         def probe(name, ap):
@@ -77,175 +95,270 @@ def tile_picked_embpos_gelu_e_kernel(tc, xT, w1, w2, pos, offs, out):
         nc.scalar.activation(warm[:, 1:2], warm[:, 0:1], GELU)
 
         planes = {}
-        x_rows = xT.rearrange("(g p j) c -> g j p c", g=PASSES, j=PACK)
-        for g in range(PASSES):
-            for j in range(PACK):
-                if g == 0 and j % 2 == 0:
-                    pair = sbuf([P, 2 * T], F32, "pair%d" % j)
-                    rows = xT[:K_PASS, :].rearrange("(p u e) c -> u p (e c)", u=2, e=2)
-                    nc.sync.dma_start(out=pair[:], in_=rows[j // 2])
-                    planes[g, j] = pair[:]
-                    planes[g, j + 1] = pair[:, T:]
-                elif g > 0:
-                    plane = sbuf([P, T], F32, "plane%d_%d" % (g, j))
-                    nc.sync.dma_start(out=plane[:], in_=x_rows[g, j])
-                    planes[g, j] = plane[:]
-                if (g, j) == (0, 0):
-                    nc.sync.dma_start(offsets[:], offs)
-        w1_raw = []
-        for g in range(PASSES):
-            w1_raw.append(sbuf([P, PACK, H], F32, "w1_raw%d" % g))
-            rows = w1[g * K_PASS : (g + 1) * K_PASS, :].rearrange("(p j) c -> p j c", j=PACK)
-            nc.sync.dma_start(out=w1_raw[g][:], in_=rows)
+        w1_raw = {}
+        x_rows = xT.rearrange("(g p j) c -> g p (j c)", g=PASSES, j=PACK)
+        w1_rows = w1.rearrange("(g p j) c -> g p j c", g=PASSES, j=PACK)
+
+        def load_x(n):
+            g, j0, rows = X_LOADS[n]
+            loaded = sbuf([P, rows * T], F32, "x%d_%d" % (g, j0))
+            nc.sync.dma_start(out=loaded[:], in_=x_rows[g][:, j0 * T : (j0 + rows) * T])
+            for r in range(rows):
+                planes[g, j0 + r] = loaded[:, r * T :]
+
+        def load_w1(n):
+            g, m0, groups = W1_LOADS[n]
+            w1_raw[n] = sbuf([P, PACK, PACK * groups], F32, "w1_raw%d" % n, n * W1_BYTES)
+            nc.sync.dma_start(out=w1_raw[n][:], in_=w1_rows[g][:, :, PACK * m0 : PACK * (m0 + groups)])
+
+        load_x(0)
+        nc.sync.dma_start(offsets[:], offs)
+        for n in range(1, len(X_LOADS) - X_BEHIND_W1):
+            load_x(n)
+        load_w1(0)
+        for n in range(len(X_LOADS) - X_BEHIND_W1, len(X_LOADS)):
+            load_x(n)
+        for n in range(1, len(W1_LOADS)):
+            load_w1(n)
+        w2_raw = sbuf([P, PACK, N], F32, "w2_raw")
         pos_rows = pos.rearrange("(p t) s -> p t s", t=PACK)
         pos_sb = {}
-        w2_raw = sbuf([P, PACK, N], F32, "w2_raw")
-        nc.sync.dma_start(out=w2_raw[:], in_=w2.rearrange("(p j) n -> p j n", j=PACK))
-        for s0, width in spans(POS_LOADS):
-            pos_sb[s0] = sbuf([P, PACK, width], F32, "pos%d" % s0)
+        for n, (s0, width) in enumerate(spans(POS_LOADS)):
+            if n == POS_AHEAD_OF_W2:
+                nc.sync.dma_start(out=w2_raw[:], in_=w2.rearrange("(p j) n -> p j n", j=PACK))
+            pos_sb[s0] = sbuf([P, PACK, width], F32, "pos%d" % s0, POS_BYTES + 16 * s0)
             nc.sync.dma_start(out=pos_sb[s0][:], in_=pos_rows[:, :, s0 : s0 + width])
 
-        picked = [sbuf([P, PACK, S], F32, "picked%d" % g) for g in range(PASSES)]
+        picked = {}
+        for g in range(PASSES):
+            for s0, width in spans(PICKED_TILES[g]):
+                picked[g, s0] = sbuf([P, PACK, width], F32, "picked%d_%d" % (g, s0))
+
+        def picked_view(g, s0, width):
+            start = max(start0 for start0, same in spans(PICKED_TILES[g]) if start0 <= s0)
+            return picked[g, start][:, :, s0 - start : s0 - start + width]
+
         x_bf = {}
         x_words = {}
         x_scales = [sbuf([P, S], U8, "x_scales%d" % g) for g in range(PASSES)]
 
-        def gather_plane(g, j, pieces):
+        def gather_plane(g, j):
+            pieces = GATHERS[g, j]
             for (s0, width), (engine, same) in zip(spans([width for engine, width in pieces]), pieces):
                 looked_up = planes[g, j].indirect(offsets[:, s0 // LIST_ROWS : (s0 + width) // LIST_ROWS])
                 if engine == "vector":
-                    nc.vector.tensor_copy(picked[g][:, j, s0 : s0 + width], looked_up)
+                    nc.vector.tensor_copy(picked_view(g, s0, width)[:, j], looked_up)
                 else:
-                    nc.scalar.activation(picked[g][:, j, s0 : s0 + width], looked_up, COPY)
+                    nc.scalar.activation(picked_view(g, s0, width)[:, j], looked_up, COPY)
 
-        def weave_x(g, s0, width, on_scalar=0, tag=None):
-            x_bf[g, s0] = sbuf([P, PACK * width], BF16, "x_bf%d_%d" % (g, s0), tag)
-            for copy, a, b in ((nc.scalar.copy, 0, on_scalar), (nc.vector.tensor_copy, on_scalar, width)):
-                if a < b:
-                    dst, src = weave_views(x_bf[g, s0][:, PACK * a : PACK * b], picked[g][:, :, s0 + a : s0 + b])
-                    copy(out=dst, in_=src)
+            probe("g%d%d" % (g, j), picked_view(g, S - 1, 1)[:, j])
 
-        def quantise_x(g, s0, width, tag=None):
-            x_words[g, s0] = sbuf([P, width], U32, "x_words%d_%d" % (g, s0), tag)
+        def weave_x(g, n, copy, tag=None):
+            s0, width = spans(X_PIECES[g])[n]
+            x_bf[g, n] = sbuf([P, PACK * width], BF16, "x_bf%d_%d" % (g, n), tag)
+            dst, src = weave_views(x_bf[g, n][:], picked_view(g, s0, width))
+            copy(out=dst, in_=src)
+            probe("xw%d%d" % (g, n), x_bf[g, n][:, 0:1])
+
+        def quantise_x(g, n, tag=None):
+            s0, width = spans(X_PIECES[g])[n]
+            x_words[g, s0] = sbuf([P, width], U32, "x_words%d_%d" % (g, n), tag)
             nc.vector.quantize_mx(
                 out=x_words[g, s0][:].bitcast(FP8X4),
                 scales=x_scales[g][:, s0 : s0 + width],
-                in_=x_bf[g, s0][:],
+                in_=x_bf[g, n][:],
             )
+            probe("xq%d%d" % (g, n), x_words[g, s0][:, 0:1])
 
-        for g in range(PASSES):
-            for j in range(PACK):
-                gather_plane(g, j, GATHERS[g, j])
-                probe("g%d%d" % (g, j), picked[g][:, j, S - 1 : S])
-            if g == 0:
-                for piece in spans(X_QUANTISE):
-                    weave_x(g, *piece)
-                for piece in spans(X_QUANTISE):
-                    quantise_x(g, *piece)
-        first, second, late = spans(LAST_PIECES)
-        weave_x(1, *first)
-        quantise_x(1, *first)
-        weave_x(1, *second, on_scalar=second[1])
-
-        w1_bf = [sbuf([P, PACK, P, PACK], BF16, "w1_bf%d" % g) for g in range(PASSES)]
+        w1_bf = {}
         w1_words = [sbuf([P, H], U32, "w1_words%d" % g) for g in range(PASSES)]
         w1_scales = [sbuf([P, H], U8, "w1_scales%d" % g) for g in range(PASSES)]
 
-        def weave_w1(g):
-            dst = w1_bf[g][:].rearrange("p t m j -> p m j t")
-            src = w1_raw[g][:].rearrange("p j (m t) -> p m j t", t=PACK)
-            split = W1_ON_VECTOR[g]
-            nc.vector.tensor_copy(out=dst[:, :split], in_=src[:, :split])
-            if split < P:
-                nc.scalar.copy(out=dst[:, split:], in_=src[:, split:])
+        def weave_w1(n):
+            g, m0, groups = W1_LOADS[n]
+            w1_bf[n] = sbuf([P, PACK, groups, PACK], BF16, "w1_bf%d" % n)
+            dst = w1_bf[n][:].rearrange("p t m j -> p m j t")
+            src = w1_raw[n][:].rearrange("p j (m t) -> p m j t", t=PACK)
+            split = W1_ON_VECTOR[n]
+            for t0, tiles in spans(W1_TILES[n]):
+                ts = slice(t0, t0 + tiles)
+                if split > 0:
+                    nc.vector.tensor_copy(out=dst[:, :split, :, ts], in_=src[:, :split, :, ts])
+                if split < groups:
+                    nc.scalar.copy(out=dst[:, split:, :, ts], in_=src[:, split:, :, ts])
 
-        def quantise_w1(g):
-            flat = w1_bf[g][:].rearrange("p t m j -> p (t m j)")
-            for c0, width in spans(W1_QUANTISE[g]):
-                cols = slice(c0, c0 + width)
+        def quantise_w1(n):
+            g, m0, groups = W1_LOADS[n]
+            for t0, tiles in spans(W1_QUANTISE[n]):
+                cols = slice(t0 * P, (t0 + tiles) * P)
                 nc.vector.quantize_mx(
                     out=w1_words[g][:, cols].bitcast(FP8X4),
                     scales=w1_scales[g][:, cols],
-                    in_=flat[:, PACK * c0 : PACK * (c0 + width)],
+                    in_=w1_bf[n][:, t0 : t0 + tiles].rearrange("p t m j -> p (t m j)"),
                 )
+            probe("w1q%d" % n, w1_words[g][:, H - P + m0 : H - P + m0 + 1])
 
-        steps = S // STEP
-        acc = [psum.tile([P, PACK, STEP], F32, name="acc%d" % b, tag="bank%d" % b) for b in range(steps)]
+        acc = {}
+        banks = 0
+        for b, (s0, width) in enumerate(spans(STEPS)):
+            sums = BANK // width
+            for t0 in range(0, PACK, sums):
+                bank = psum.tile([P, sums, width], F32, name="acc%d" % banks, tag="bank%d" % banks)
+                banks = banks + 1
+                for t in range(t0, t0 + sums):
+                    acc[b, t] = (bank, t - t0, sums)
 
         def first_product_pass(b, g, t, start, stop):
+            s0, width = spans(STEPS)[b]
             cols = slice(t * P, (t + 1) * P)
-            entries = slice(b * STEP, (b + 1) * STEP)
-            piece = max(s0 for s0, width in spans((X_QUANTISE, LAST_PIECES)[g]) if s0 <= b * STEP)
+            piece = max(start0 for start0, same in spans(X_PIECES[g]) if start0 <= s0)
+            bank, place, sums = acc[b, t]
             nc.tensor.matmul_mx(
-                out=acc[b][:, t, :],
+                out=bank[:, place, :],
                 lhsT=w1_words[g][:, cols].bitcast(FP8X4),
                 lhsT_scale=w1_scales[g][:, cols],
-                rhs=x_words[g, piece][:, b * STEP - piece : (b + 1) * STEP - piece].bitcast(FP8X4),
-                rhs_scale=x_scales[g][:, entries],
+                rhs=x_words[g, piece][:, s0 - piece : s0 + width - piece].bitcast(FP8X4),
+                rhs_scale=x_scales[g][:, s0 : s0 + width],
                 start=start,
                 stop=stop,
             )
 
-        for g in range(PASSES):
-            weave_w1(g)
-            quantise_w1(g)
-            probe("w1q%d" % g, w1_words[g][:, H - 1 : H])
-            for b in range(OPEN_BANKS):
+        def open_pass(g):
+            for b in range(OPEN_STEPS):
+                tiles = list(range(PACK))
+                if g > 0 and b > 0:
+                    tiles = list(reversed(tiles))
+                for t in tiles:
+                    first_product_pass(b, g, t, g == 0 and t == tiles[0], g == PASSES - 1 and t == tiles[-1])
+
+
+        def closing_pass(steps):
+            for b in steps:
                 for t in range(PACK):
-                    first_product_pass(b, g, t, (g, t) == (0, 0), (g, t) == (PASSES - 1, PACK - 1))
-        quantise_x(1, *second, tag="w1_bf1")
-        weave_x(1, *late, on_scalar=late[1], tag="w1_raw1")
-        quantise_x(1, *late)
-        for b in range(OPEN_BANKS, steps):
-            for t in range(PACK):
+                    bank, place, sums = acc[b, t]
+                    first_product_pass(b, PASSES - 1, t, False, place == sums - 1)
+
+        def closed_step(b):
+            for t in reversed(range(PACK)):
                 for g in reversed(range(PASSES)):
                     first_product_pass(b, g, t, g == PASSES - 1, g == 0)
 
         w2_bf = sbuf([P, N * PACK], BF16, "w2_bf")
-        w2_words = sbuf([P, N], U32, "w2_words")
         w2_scales = sbuf([P, N], U8, "w2_scales")
         h_bf = sbuf([P, S * PACK], BF16, "h_bf")
-        h_words = sbuf([P, S], U32, "h_words")
         h_scales = sbuf([P, S], U8, "h_scales")
 
         def hidden(b):
-            s0 = b * STEP
+            s0, width = spans(STEPS)[b]
             pos0 = max(start for start in pos_sb if start <= s0)
-            pre = sbuf([P, PACK, STEP], F32, "pre%d" % b)
-            nc.vector.tensor_tensor(pre[:], acc[b][:], pos_sb[pos0][:, :, s0 - pos0 : s0 - pos0 + STEP], ADD)
-            probe("add%d" % b, pre[:, 0, 0:1])
-            dst, src = weave_views(h_bf[:, PACK * s0 : PACK * (s0 + STEP)], pre[:])
+            pre = sbuf([P, PACK, width], F32, "pre%d" % b, PRE_BYTES + 2048 * (COPY_BEHIND_GELU - b) if b in (COPY_BEHIND_GELU - 1, COPY_BEHIND_GELU) else None)
+            sums = acc[b, 0][2]
+            for t0 in range(0, PACK, sums):
+                ts = slice(t0, t0 + sums)
+                nc.vector.tensor_tensor(
+                    pre[:, ts], acc[b, t0][0][:], pos_sb[pos0][:, ts, s0 - pos0 : s0 - pos0 + width], ADD
+                )
+            probe("add%d" % b, pre[:, PACK - 1, 0:1])
+            dst, src = weave_views(h_bf[:, PACK * s0 : PACK * (s0 + width)], pre[:])
             nc.scalar.activation(dst, src, GELU)
             probe("gelu%d" % b, h_bf[:, PACK * s0 : PACK * s0 + 1])
 
-        def second_product(b, s0, width):
+        def weave_w2(copy):
+            dst, src = weave_views(w2_bf[:], w2_raw[:])
+            copy(out=dst, in_=src)
+
+        def quantise_w2(tag=None):
+            words = sbuf([P, N], U32, "w2_words", tag)
+            nc.vector.quantize_mx(out=words[:].bitcast(FP8X4), scales=w2_scales[:], in_=w2_bf[:])
+            return words
+
+        res = {}
+
+        def second_product(b, w2_words, tag=None):
+            s0, width = spans(OUT_STEPS)[b]
             cols = slice(s0, s0 + width)
+            h_words = sbuf([P, width], U32, "h_words%d" % b, tag)
             nc.vector.quantize_mx(
-                out=h_words[:, cols].bitcast(FP8X4),
+                out=h_words[:].bitcast(FP8X4),
                 scales=h_scales[:, cols],
                 in_=h_bf[:, PACK * s0 : PACK * (s0 + width)],
             )
-            res = psum.tile([P, width], F32, name="res%d" % b, tag="bank%d" % b)
+            res[b] = psum.tile([P, width], F32, name="res%d" % b, tag="bank%d" % b)
             nc.tensor.matmul_mx(
-                out=res[:],
+                out=res[b][:],
                 lhsT=w2_words[:].bitcast(FP8X4),
                 lhsT_scale=w2_scales[:],
-                rhs=h_words[:, cols].bitcast(FP8X4),
+                rhs=h_words[:].bitcast(FP8X4),
                 rhs_scale=h_scales[:, cols],
                 start=True,
                 stop=True,
             )
-            staged = sbuf([P, width], F32, "staged%d" % b)
-            if b in COPIES_ON_VECTOR:
-                nc.vector.tensor_copy(out=staged[:], in_=res[:])
-            else:
-                nc.scalar.copy(out=staged[:], in_=res[:])
-            nc.sync.dma_start(out=out[:, cols], in_=staged[:])
 
-        for b in range(steps):
+        staged = {}
+
+        def stage(n, tag=None):
+            s0, width = spans(STORES)[n]
+            staged[s0] = sbuf([P, width], F32, "staged%d" % n, tag)
+
+        def leave_psum(b, copy):
+            s0, width = spans(OUT_STEPS)[b]
+            start = max(start0 for start0 in staged if start0 <= s0)
+            copy(out=staged[start][:, s0 - start : s0 - start + width], in_=res[b][:])
+            probe("copy%d" % b, staged[start][:, s0 - start : s0 - start + 1])
+
+        def store(n):
+            s0, width = spans(STORES)[n]
+            nc.sync.dma_start(out=out[:, s0 : s0 + width], in_=staged[s0][:])
+
+        for j in range(PACK):
+            gather_plane(0, j)
+        weave_x(0, 0, nc.vector.tensor_copy)
+        weave_x(0, 1, nc.vector.tensor_copy)
+        weave_x(0, 2, nc.scalar.copy)
+        for n in range(len(X_PIECES[0])):
+            quantise_x(0, n)
+        for j in range(PACK):
+            gather_plane(1, j)
+        weave_x(1, 0, nc.vector.tensor_copy)
+        weave_x(1, 1, nc.vector.tensor_copy)
+        quantise_x(1, 0)
+        quantise_x(1, 1)
+        weave_x(1, 2, nc.scalar.copy)
+        weave_x(1, 3, nc.scalar.copy)
+        weave_x(1, 4, nc.scalar.copy)
+        weave_w1(0)
+        quantise_w1(0)
+        open_pass(0)
+        quantise_x(1, 2, tag=0)
+        weave_w1(1)
+        quantise_w1(1)
+        open_pass(1)
+        quantise_x(1, 3, tag=W1_BYTES + 2048)
+        weave_x(1, 5, nc.scalar.copy, tag=W1_BYTES)
+        quantise_x(1, 4, tag=W1_BYTES + 4096)
+        quantise_x(1, 5)
+        for b in range(OPEN_STEPS, len(STEPS)):
+            closed_step(b)
+        for b in range(len(STEPS)):
             hidden(b)
-        dst, src = weave_views(w2_bf[:], w2_raw[:])
-        nc.scalar.copy(out=dst, in_=src)
-        nc.vector.quantize_mx(out=w2_words[:].bitcast(FP8X4), scales=w2_scales[:], in_=w2_bf[:])
-        for b, (s0, width) in enumerate(spans(OUT_STEPS)):
-            second_product(b, s0, width)
+        weave_w2(nc.scalar.copy)
+        w2_words = quantise_w2()
+        stage(0, PRE_BYTES)
+        stage(1, PRE_BYTES + 1024)
+        for n in range(2, len(STORES)):
+            stage(n)
+        second_product(0, w2_words, POS_BYTES + 16 * H_BEHIND)
+        leave_psum(0, nc.scalar.copy)
+        store(0)
+        second_product(1, w2_words, POS_BYTES + 16 * H_BEHIND + 1024)
+        leave_psum(1, nc.scalar.copy)
+        store(1)
+        second_product(2, w2_words)
+        leave_psum(2, nc.vector.tensor_copy)
+        store(2)
+        second_product(3, w2_words)
+        leave_psum(3, nc.vector.tensor_copy)
+        store(3)
+        second_product(4, w2_words)
+        leave_psum(4, nc.scalar.copy)
+        store(4)

@@ -27,7 +27,7 @@ WALK = 4
 X_LOADS = ((0, 0, 2), (0, 2, 2), (1, 0, 2), (1, 2, 1), (1, 3, 1))
 PLANE_5 = (("vector", 1024),)
 PLANE_6 = (("vector", 256), ("scalar", 768))
-LAST_PLANE = (("vector", 128), ("vector", 256), ("scalar", 128), ("scalar", 512))
+LAST_PLANE = (("vector", 128), ("vector", 256), ("scalar", 256), ("scalar", 384))
 GATHERS = {
     (0, 0): (("scalar", 1024),),
     (0, 1): (("vector", 1024),),
@@ -46,16 +46,19 @@ W1_QUANTISE = ((2, 2), (2, 1, 1))
 POS_BYTES = 2 * W1_BYTES
 PRE_BYTES = 4 * W1_BYTES
 COPY_BEHIND_GELU = 6
-X_PIECES = ((512, 128, 384), (128, 128, 256, 256, 128, 128))
+X_PIECES = ((512, 128, 384), (128, 256, 256, 384))
 W1_LOADS = ((0, 0, 128), (1, 0, 128))
 W1_ON_VECTOR = (128, 80)
 POS_LOADS = (256, 256, 256, 128, 128)
 STEPS = (128, 128, 128, 128, 128, 128, 128, 128)
 POS_AHEAD_OF_W2 = 0
+GPSIMD_STEPS = ()
 STORES = (256, 256, 256, 128, 128)
 H_BEHIND = 512
 OPEN_STEPS = 3
 OUT_STEPS = (256, 256, 256, 128, 128)
+GELU_ORDER = (0, 1, 2, 3, 4, 5, 6, 7)
+COPIES_ON_VECTOR = (2, 3)
 PROBES = ()
 
 
@@ -226,17 +229,10 @@ def tile_picked_embpos_gelu_e_kernel(tc, xT, w1, w2, pos, offs, out):
         def open_pass(g):
             for b in range(OPEN_STEPS):
                 tiles = list(range(PACK))
-                if g > 0 and b > 0:
+                if g > 0 and b > 1:
                     tiles = list(reversed(tiles))
                 for t in tiles:
                     first_product_pass(b, g, t, g == 0 and t == tiles[0], g == PASSES - 1 and t == tiles[-1])
-
-
-        def closing_pass(steps):
-            for b in steps:
-                for t in range(PACK):
-                    bank, place, sums = acc[b, t]
-                    first_product_pass(b, PASSES - 1, t, False, place == sums - 1)
 
         def closed_step(b):
             for t in reversed(range(PACK)):
@@ -248,18 +244,24 @@ def tile_picked_embpos_gelu_e_kernel(tc, xT, w1, w2, pos, offs, out):
         h_bf = sbuf([P, S * PACK], BF16, "h_bf")
         h_scales = sbuf([P, S], U8, "h_scales")
 
-        def hidden(b):
+        pre = {}
+
+        def add_pos(b):
             s0, width = spans(STEPS)[b]
             pos0 = max(start for start in pos_sb if start <= s0)
-            pre = sbuf([P, PACK, width], F32, "pre%d" % b, PRE_BYTES + 2048 * (COPY_BEHIND_GELU - b) if b in (COPY_BEHIND_GELU - 1, COPY_BEHIND_GELU) else None)
-            sums = acc[b, 0][2]
-            for t0 in range(0, PACK, sums):
-                ts = slice(t0, t0 + sums)
-                nc.vector.tensor_tensor(
-                    pre[:, ts], acc[b, t0][0][:], pos_sb[pos0][:, ts, s0 - pos0 : s0 - pos0 + width], ADD
-                )
-            probe("add%d" % b, pre[:, PACK - 1, 0:1])
-            dst, src = weave_views(h_bf[:, PACK * s0 : PACK * (s0 + width)], pre[:])
+            pre[b] = sbuf([P, PACK, width], F32, "pre%d" % b, PRE_BYTES + 2048 * b)
+            place = pos_sb[pos0][:, :, s0 - pos0 : s0 - pos0 + width]
+            if b in GPSIMD_STEPS:
+                sums = sbuf([P, PACK, width], F32, "sums%d" % b)
+                nc.scalar.copy(out=sums[:], in_=acc[b, 0][0][:])
+                nc.gpsimd.tensor_tensor(pre[b][:], sums[:], place, ADD)
+            else:
+                nc.vector.tensor_tensor(pre[b][:], acc[b, 0][0][:], place, ADD)
+            probe("add%d" % b, pre[b][:, PACK - 1, 0:1])
+
+        def hidden(b):
+            s0, width = spans(STEPS)[b]
+            dst, src = weave_views(h_bf[:, PACK * s0 : PACK * (s0 + width)], pre[b][:])
             nc.scalar.activation(dst, src, GELU)
             probe("gelu%d" % b, h_bf[:, PACK * s0 : PACK * s0 + 1])
 
@@ -325,7 +327,6 @@ def tile_picked_embpos_gelu_e_kernel(tc, xT, w1, w2, pos, offs, out):
         quantise_x(1, 1)
         weave_x(1, 2, nc.scalar.copy)
         weave_x(1, 3, nc.scalar.copy)
-        weave_x(1, 4, nc.scalar.copy)
         weave_w1(0)
         quantise_w1(0)
         open_pass(0)
@@ -333,32 +334,26 @@ def tile_picked_embpos_gelu_e_kernel(tc, xT, w1, w2, pos, offs, out):
         weave_w1(1)
         quantise_w1(1)
         open_pass(1)
-        quantise_x(1, 3, tag=W1_BYTES + 2048)
-        weave_x(1, 5, nc.scalar.copy, tag=W1_BYTES)
-        quantise_x(1, 4, tag=W1_BYTES + 4096)
-        quantise_x(1, 5)
-        for b in range(OPEN_STEPS, len(STEPS)):
-            closed_step(b)
-        for b in range(len(STEPS)):
-            hidden(b)
+        quantise_x(1, 3, tag=W1_BYTES)
         weave_w2(nc.scalar.copy)
         w2_words = quantise_w2()
-        stage(0, PRE_BYTES)
-        stage(1, PRE_BYTES + 1024)
+        for b in range(OPEN_STEPS, len(STEPS)):
+            closed_step(b)
+        for b in GPSIMD_STEPS:
+            add_pos(b)
+        for b in range(len(STEPS)):
+            if b not in GPSIMD_STEPS:
+                add_pos(b)
+        for b in GELU_ORDER:
+            hidden(b)
+        stage(0, PRE_BYTES + 2048 * COPY_BEHIND_GELU)
+        stage(1, PRE_BYTES + 2048 * COPY_BEHIND_GELU + 1024)
         for n in range(2, len(STORES)):
             stage(n)
         second_product(0, w2_words, POS_BYTES + 16 * H_BEHIND)
-        leave_psum(0, nc.scalar.copy)
-        store(0)
         second_product(1, w2_words, POS_BYTES + 16 * H_BEHIND + 1024)
-        leave_psum(1, nc.scalar.copy)
-        store(1)
-        second_product(2, w2_words)
-        leave_psum(2, nc.vector.tensor_copy)
-        store(2)
-        second_product(3, w2_words)
-        leave_psum(3, nc.vector.tensor_copy)
-        store(3)
-        second_product(4, w2_words)
-        leave_psum(4, nc.scalar.copy)
-        store(4)
+        for n in range(2, len(STORES)):
+            second_product(n, w2_words)
+        for n in range(len(STORES)):
+            leave_psum(n, nc.vector.tensor_copy if n in COPIES_ON_VECTOR else nc.scalar.copy)
+            store(n)

@@ -26,8 +26,8 @@ WALK = 4
 
 X_LOADS = ((0, 0, 2), (0, 2, 2), (1, 0, 2), (1, 2, 1), (1, 3, 1))
 PLANE_5 = (("vector", 1024),)
-PLANE_6 = (("vector", 256), ("scalar", 768))
-LAST_PLANE = (("vector", 128), ("vector", 256), ("scalar", 256), ("scalar", 384))
+PLANE_6 = (("vector", 128), ("vector", 128), ("scalar", 768))
+LAST_PLANE = (("placed", 256), ("vector", 128), ("scalar", 256), ("scalar", 384))
 GATHERS = {
     (0, 0): (("scalar", 1024),),
     (0, 1): (("vector", 1024),),
@@ -46,19 +46,21 @@ W1_QUANTISE = ((2, 2), (2, 1, 1))
 POS_BYTES = 2 * W1_BYTES
 PRE_BYTES = 4 * W1_BYTES
 COPY_BEHIND_GELU = 6
-X_PIECES = ((512, 128, 384), (128, 256, 256, 384))
+FIRST_PASS_ON_VECTOR = 64
+X_PIECES = ((512, 512), (256, 128, 256, 384))
 W1_LOADS = ((0, 0, 128), (1, 0, 128))
 W1_ON_VECTOR = (128, 80)
 POS_LOADS = (256, 256, 256, 128, 128)
 STEPS = (128, 128, 128, 128, 128, 128, 128, 128)
 POS_AHEAD_OF_W2 = 0
 GPSIMD_STEPS = ()
-STORES = (256, 256, 256, 128, 128)
+STORES = (128, 128, 256, 256, 128, 128)
 H_BEHIND = 512
 OPEN_STEPS = 3
 OUT_STEPS = (256, 256, 256, 128, 128)
 GELU_ORDER = (0, 1, 2, 3, 4, 5, 6, 7)
-COPIES_ON_VECTOR = (2, 3)
+COPIES_ON_VECTOR = (3, 4)
+EARLY_BEHIND = 4
 PROBES = ()
 
 
@@ -147,20 +149,25 @@ def tile_picked_embpos_gelu_e_kernel(tc, xT, w1, w2, pos, offs, out):
 
         def gather_plane(g, j):
             pieces = GATHERS[g, j]
-            for (s0, width), (engine, same) in zip(spans([width for engine, width in pieces]), pieces):
+            cuts = list(zip(spans([width for engine, width in pieces]), pieces))
+            for (s0, width), (engine, same) in sorted(cuts, key=lambda cut: cut[1][0] == "placed"):
                 looked_up = planes[g, j].indirect(offsets[:, s0 // LIST_ROWS : (s0 + width) // LIST_ROWS])
-                if engine == "vector":
+                if engine == "placed":
+                    nc.vector.tensor_copy(x_bf[g, 0][:].rearrange("p (c j) -> p c j", j=PACK)[:, :, j], looked_up)
+                elif engine == "vector":
                     nc.vector.tensor_copy(picked_view(g, s0, width)[:, j], looked_up)
                 else:
                     nc.scalar.activation(picked_view(g, s0, width)[:, j], looked_up, COPY)
 
             probe("g%d%d" % (g, j), picked_view(g, S - 1, 1)[:, j])
 
-        def weave_x(g, n, copy, tag=None):
+        def weave_x(g, n, copy, tag=None, rows=PACK, part=None):
             s0, width = spans(X_PIECES[g])[n]
-            x_bf[g, n] = sbuf([P, PACK * width], BF16, "x_bf%d_%d" % (g, n), tag)
-            dst, src = weave_views(x_bf[g, n][:], picked_view(g, s0, width))
-            copy(out=dst, in_=src)
+            if (g, n) not in x_bf:
+                x_bf[g, n] = sbuf([P, PACK * width], BF16, "x_bf%d_%d" % (g, n), tag)
+            first, last = part or (0, width)
+            dst, src = weave_views(x_bf[g, n][:, PACK * first : PACK * last], picked_view(g, s0 + first, last - first))
+            copy(out=dst[:, :, :rows], in_=src[:, :, :rows])
             probe("xw%d%d" % (g, n), x_bf[g, n][:, 0:1])
 
         def quantise_x(g, n, tag=None):
@@ -229,7 +236,7 @@ def tile_picked_embpos_gelu_e_kernel(tc, xT, w1, w2, pos, offs, out):
         def open_pass(g):
             for b in range(OPEN_STEPS):
                 tiles = list(range(PACK))
-                if g > 0 and b > 1:
+                if g > 0 and b > 0:
                     tiles = list(reversed(tiles))
                 for t in tiles:
                     first_product_pass(b, g, t, g == 0 and t == tiles[0], g == PASSES - 1 and t == tiles[-1])
@@ -302,11 +309,12 @@ def tile_picked_embpos_gelu_e_kernel(tc, xT, w1, w2, pos, offs, out):
             s0, width = spans(STORES)[n]
             staged[s0] = sbuf([P, width], F32, "staged%d" % n, tag)
 
-        def leave_psum(b, copy):
-            s0, width = spans(OUT_STEPS)[b]
-            start = max(start0 for start0 in staged if start0 <= s0)
-            copy(out=staged[start][:, s0 - start : s0 - start + width], in_=res[b][:])
-            probe("copy%d" % b, staged[start][:, s0 - start : s0 - start + 1])
+        def leave_psum(n, copy):
+            s0, width = spans(STORES)[n]
+            b = max(b0 for b0, (start0, same) in enumerate(spans(OUT_STEPS)) if start0 <= s0)
+            start = spans(OUT_STEPS)[b][0]
+            copy(out=staged[s0][:], in_=res[b][:, s0 - start : s0 - start + width])
+            probe("copy%d" % n, staged[s0][:, 0:1])
 
         def store(n):
             s0, width = spans(STORES)[n]
@@ -315,13 +323,15 @@ def tile_picked_embpos_gelu_e_kernel(tc, xT, w1, w2, pos, offs, out):
         for j in range(PACK):
             gather_plane(0, j)
         weave_x(0, 0, nc.vector.tensor_copy)
-        weave_x(0, 1, nc.vector.tensor_copy)
-        weave_x(0, 2, nc.scalar.copy)
+        weave_x(0, 1, nc.vector.tensor_copy, part=(0, FIRST_PASS_ON_VECTOR))
+        weave_x(0, 1, nc.scalar.copy, part=(FIRST_PASS_ON_VECTOR, 512))
         for n in range(len(X_PIECES[0])):
             quantise_x(0, n)
-        for j in range(PACK):
+        for j in range(PACK - 1):
             gather_plane(1, j)
-        weave_x(1, 0, nc.vector.tensor_copy)
+        weave_x(1, 0, nc.vector.tensor_copy, rows=PACK - 1, part=(0, P))
+        weave_x(1, 0, nc.vector.tensor_copy, rows=PACK - 1, part=(P, 2 * P))
+        gather_plane(1, PACK - 1)
         weave_x(1, 1, nc.vector.tensor_copy)
         quantise_x(1, 0)
         quantise_x(1, 1)
@@ -339,20 +349,21 @@ def tile_picked_embpos_gelu_e_kernel(tc, xT, w1, w2, pos, offs, out):
         w2_words = quantise_w2()
         for b in range(OPEN_STEPS, len(STEPS)):
             closed_step(b)
-        for b in GPSIMD_STEPS:
+        for b in range(EARLY_BEHIND):
             add_pos(b)
-        for b in range(len(STEPS)):
-            if b not in GPSIMD_STEPS:
-                add_pos(b)
-        for b in GELU_ORDER:
             hidden(b)
-        stage(0, PRE_BYTES + 2048 * COPY_BEHIND_GELU)
-        stage(1, PRE_BYTES + 2048 * COPY_BEHIND_GELU + 1024)
-        for n in range(2, len(STORES)):
-            stage(n)
-        second_product(0, w2_words, POS_BYTES + 16 * H_BEHIND)
-        second_product(1, w2_words, POS_BYTES + 16 * H_BEHIND + 1024)
-        for n in range(2, len(STORES)):
+        second_product(0, w2_words)
+        for b in range(EARLY_BEHIND, len(STEPS)):
+            add_pos(b)
+            hidden(b)
+        stage(0, POS_BYTES + 16 * 896)
+        stage(1, POS_BYTES + 16 * 896 + 512)
+        stage(2, PRE_BYTES + 2048 * COPY_BEHIND_GELU + 1024)
+        stage(3, PRE_BYTES + 2048 * 7)
+        stage(4, PRE_BYTES + 2048 * 7 + 1024)
+        stage(5)
+        second_product(1, w2_words, POS_BYTES + 16 * H_BEHIND)
+        for n in range(2, len(OUT_STEPS)):
             second_product(n, w2_words)
         for n in range(len(STORES)):
             leave_psum(n, nc.vector.tensor_copy if n in COPIES_ON_VECTOR else nc.scalar.copy)

@@ -54,13 +54,13 @@ POS_LOADS = (256, 256, 256, 128, 128)
 STEPS = (128, 128, 128, 128, 128, 128, 128, 128)
 POS_AHEAD_OF_W2 = 0
 GPSIMD_STEPS = ()
-STORES = (128, 128, 256, 256, 128, 128)
+STORES = (256, 128, 128, 256, 128, 128)
 H_BEHIND = 512
 OPEN_STEPS = 3
 OUT_STEPS = (256, 256, 256, 128, 128)
 GELU_ORDER = (0, 1, 2, 3, 4, 5, 6, 7)
 COPIES_ON_VECTOR = (3, 4)
-EARLY_BEHIND = 4
+EARLY_BEHIND = 3
 PROBES = ()
 
 
@@ -256,20 +256,19 @@ def tile_picked_embpos_gelu_e_kernel(tc, xT, w1, w2, pos, offs, out):
         def add_pos(b):
             s0, width = spans(STEPS)[b]
             pos0 = max(start for start in pos_sb if start <= s0)
-            pre[b] = sbuf([P, PACK, width], F32, "pre%d" % b, PRE_BYTES + 2048 * b)
+            pre[b] = sbuf([P, PACK * width], F32, "pre%d" % b, PRE_BYTES + 2048 * b)
             place = pos_sb[pos0][:, :, s0 - pos0 : s0 - pos0 + width]
-            if b in GPSIMD_STEPS:
-                sums = sbuf([P, PACK, width], F32, "sums%d" % b)
-                nc.scalar.copy(out=sums[:], in_=acc[b, 0][0][:])
-                nc.gpsimd.tensor_tensor(pre[b][:], sums[:], place, ADD)
-            else:
-                nc.vector.tensor_tensor(pre[b][:], acc[b, 0][0][:], place, ADD)
-            probe("add%d" % b, pre[b][:, PACK - 1, 0:1])
+            nc.vector.tensor_tensor(
+                pre[b][:].rearrange("p (c t i) -> p c t i", t=PACK, i=2),
+                acc[b, 0][0][:].rearrange("p t (c i) -> p c t i", i=2),
+                place.rearrange("p t (c i) -> p c t i", i=2),
+                ADD,
+            )
 
         def hidden(b):
             s0, width = spans(STEPS)[b]
-            dst, src = weave_views(h_bf[:, PACK * s0 : PACK * (s0 + width)], pre[b][:])
-            nc.scalar.activation(dst, src, GELU)
+            dst = h_bf[:, PACK * s0 : PACK * (s0 + width)].rearrange("p (c i t) -> p c t i", t=PACK, i=2)
+            nc.scalar.activation(dst, pre[b][:].rearrange("p (c t i) -> p c t i", t=PACK, i=2), GELU)
             probe("gelu%d" % b, h_bf[:, PACK * s0 : PACK * s0 + 1])
 
         def weave_w2(copy):
@@ -347,24 +346,28 @@ def tile_picked_embpos_gelu_e_kernel(tc, xT, w1, w2, pos, offs, out):
         quantise_x(1, 3, tag=W1_BYTES)
         weave_w2(nc.scalar.copy)
         w2_words = quantise_w2()
-        for b in range(OPEN_STEPS, len(STEPS)):
+        for b in range(OPEN_STEPS, 5):
             closed_step(b)
         for b in range(EARLY_BEHIND):
             add_pos(b)
             hidden(b)
         second_product(0, w2_words)
+        for b in range(5, len(STEPS)):
+            closed_step(b)
+        stage(0)
+        leave_psum(0, nc.scalar.copy)
+        store(0)
         for b in range(EARLY_BEHIND, len(STEPS)):
             add_pos(b)
             hidden(b)
-        stage(0, POS_BYTES + 16 * 896)
         stage(1, POS_BYTES + 16 * 896 + 512)
-        stage(2, PRE_BYTES + 2048 * COPY_BEHIND_GELU + 1024)
+        stage(2, POS_BYTES + 16 * 896 + 1024)
         stage(3, PRE_BYTES + 2048 * 7)
         stage(4, PRE_BYTES + 2048 * 7 + 1024)
         stage(5)
         second_product(1, w2_words, POS_BYTES + 16 * H_BEHIND)
         for n in range(2, len(OUT_STEPS)):
             second_product(n, w2_words)
-        for n in range(len(STORES)):
+        for n in range(1, len(STORES)):
             leave_psum(n, nc.vector.tensor_copy if n in COPIES_ON_VECTOR else nc.scalar.copy)
             store(n)

from contextlib import ExitStack

import concourse.mybir as mybir

K, T, S, H, N = 1024, 2048, 1024, 512, 128
FLOPS = 2 * S * (K * H + H * N)

F32 = mybir.dt.float32
BF16 = mybir.dt.bfloat16
U32 = mybir.dt.uint32
U16 = mybir.dt.uint16
U8 = mybir.dt.uint8
FP8X4 = mybir.dt.float8_e4m3fn_x4
GELU = mybir.ActivationFunctionType.Gelu_apprx_tanh
COPY = mybir.ActivationFunctionType.Copy
ADD = mybir.AluOpType.add

P = 128
PACK = 4
K_PASS = P * PACK
PASSES = K // K_PASS
LIST_ROWS = 16
ALIGN = 64
BANK = 512
WALK = 4

X_LOADS = ((0, 0, 2), (0, 2, 2), (1, 0, 2), (1, 2, 1), (1, 3, 1))
PLANE_5 = (("vector", 1024),)
PLANE_6 = (("vector", 128), ("vector", 128), ("scalar", 768))
LAST_PLANE = (("placed", 256), ("vector", 128), ("scalar", 256), ("scalar", 384))
GATHERS = {
    (0, 0): (("scalar", 1024),),
    (0, 1): (("vector", 1024),),
    (0, 2): (("scalar", 1024),),
    (0, 3): (("vector", 1024),),
    (1, 0): (("scalar", 1024),),
    (1, 1): PLANE_5,
    (1, 2): PLANE_6,
    (1, 3): LAST_PLANE,
}
X_BEHIND_W1 = 0
PICKED_TILES = ((1024,), (1024,))
W1_BYTES = 8192
W1_TILES = ((2, 2), (2, 2))
W1_QUANTISE = ((2, 2), (2, 1, 1))
POS_BYTES = 2 * W1_BYTES
PRE_BYTES = 4 * W1_BYTES
COPY_BEHIND_GELU = 6
FIRST_PASS_ON_VECTOR = 64
X_PIECES = ((512, 512), (256, 128, 256, 384))
W1_LOADS = ((0, 0, 128), (1, 0, 128))
W1_ON_VECTOR = (128, 80)
POS_LOADS = (256, 256, 256, 128, 128)
STEPS = (128, 128, 128, 128, 128, 128, 128, 128)
POS_AHEAD_OF_W2 = 0
GPSIMD_STEPS = ()
STORES = (256, 128, 128, 256, 128, 128)
H_BEHIND = 512
OPEN_STEPS = 3
OUT_STEPS = (256, 256, 256, 128, 128)
GELU_ORDER = (0, 1, 2, 3, 4, 5, 6, 7)
COPIES_ON_VECTOR = (3, 4)
EARLY_BEHIND = 3
PROBES = ()


def spans(widths):
    return [(sum(widths[:i]), width) for i, width in enumerate(widths)]


def weave_views(dst, src):
    return (
        dst.rearrange("p (c i j) -> p c j i", i=WALK, j=PACK),
        src.rearrange("p j (c i) -> p c j i", i=WALK),
    )


def tile_picked_embpos_gelu_e_kernel(tc, xT, w1, w2, pos, offs, out):
    nc = tc.nc
    with ExitStack() as ctx:
        lists = ctx.enter_context(tc.tile_pool(name="lists", bufs=1))
        sb = ctx.enter_context(tc.tile_pool(name="sb", bufs=1))
        psum = ctx.enter_context(tc.psum_pool(name="psum", bufs=1))

        shared = ctx.enter_context(tc.tile_pool(name="shared", bufs=1))

        def sbuf(shape, dtype, name, tag=None):
            if isinstance(tag, int):
                return shared.tile(shape, dtype, name=name, tag=name, align_bytes=ALIGN, offset=tag)
            return sb.tile(shape, dtype, name=name, tag=tag or name, align_bytes=ALIGN)

        def probe(name, ap):
            if name in PROBES:
                mark = sbuf([P, 1], ap.dtype, "probe_" + name)
                nc.gpsimd.tensor_copy(mark[:], ap)

        offsets = lists.tile([P, S // LIST_ROWS], U16, name="offsets")
        warm = sbuf([P, 2], F32, "warm")
        nc.gpsimd.memset(warm[:, 0:1], 0.0)
        nc.scalar.activation(warm[:, 1:2], warm[:, 0:1], GELU)

        planes = {}
        w1_raw = {}
        x_rows = xT.rearrange("(g p j) c -> g p (j c)", g=PASSES, j=PACK)
        w1_rows = w1.rearrange("(g p j) c -> g p j c", g=PASSES, j=PACK)

        def load_x(n):
            g, j0, rows = X_LOADS[n]
            loaded = sbuf([P, rows * T], F32, "x%d_%d" % (g, j0))
            nc.sync.dma_start(out=loaded[:], in_=x_rows[g][:, j0 * T : (j0 + rows) * T])
            for r in range(rows):
                planes[g, j0 + r] = loaded[:, r * T :]

        def load_w1(n):
            g, m0, groups = W1_LOADS[n]
            w1_raw[n] = sbuf([P, PACK, PACK * groups], F32, "w1_raw%d" % n, n * W1_BYTES)
            nc.sync.dma_start(out=w1_raw[n][:], in_=w1_rows[g][:, :, PACK * m0 : PACK * (m0 + groups)])

        load_x(0)
        nc.sync.dma_start(offsets[:], offs)
        for n in range(1, len(X_LOADS) - X_BEHIND_W1):
            load_x(n)
        load_w1(0)
        for n in range(len(X_LOADS) - X_BEHIND_W1, len(X_LOADS)):
            load_x(n)
        for n in range(1, len(W1_LOADS)):
            load_w1(n)
        w2_raw = sbuf([P, PACK, N], F32, "w2_raw")
        pos_rows = pos.rearrange("(p t) s -> p t s", t=PACK)
        pos_sb = {}
        for n, (s0, width) in enumerate(spans(POS_LOADS)):
            if n == POS_AHEAD_OF_W2:
                nc.sync.dma_start(out=w2_raw[:], in_=w2.rearrange("(p j) n -> p j n", j=PACK))
            pos_sb[s0] = sbuf([P, PACK, width], F32, "pos%d" % s0, POS_BYTES + 16 * s0)
            nc.sync.dma_start(out=pos_sb[s0][:], in_=pos_rows[:, :, s0 : s0 + width])

        picked = {}
        for g in range(PASSES):
            for s0, width in spans(PICKED_TILES[g]):
                picked[g, s0] = sbuf([P, PACK, width], F32, "picked%d_%d" % (g, s0))

        def picked_view(g, s0, width):
            start = max(start0 for start0, same in spans(PICKED_TILES[g]) if start0 <= s0)
            return picked[g, start][:, :, s0 - start : s0 - start + width]

        x_bf = {}
        x_words = {}
        x_scales = [sbuf([P, S], U8, "x_scales%d" % g) for g in range(PASSES)]

        def gather_plane(g, j):
            pieces = GATHERS[g, j]
            cuts = list(zip(spans([width for engine, width in pieces]), pieces))
            for (s0, width), (engine, same) in sorted(cuts, key=lambda cut: cut[1][0] == "placed"):
                looked_up = planes[g, j].indirect(offsets[:, s0 // LIST_ROWS : (s0 + width) // LIST_ROWS])
                if engine == "placed":
                    nc.vector.tensor_copy(x_bf[g, 0][:].rearrange("p (c j) -> p c j", j=PACK)[:, :, j], looked_up)
                elif engine == "vector":
                    nc.vector.tensor_copy(picked_view(g, s0, width)[:, j], looked_up)
                else:
                    nc.scalar.activation(picked_view(g, s0, width)[:, j], looked_up, COPY)

            probe("g%d%d" % (g, j), picked_view(g, S - 1, 1)[:, j])

        def weave_x(g, n, copy, tag=None, rows=PACK, part=None):
            s0, width = spans(X_PIECES[g])[n]
            if (g, n) not in x_bf:
                x_bf[g, n] = sbuf([P, PACK * width], BF16, "x_bf%d_%d" % (g, n), tag)
            first, last = part or (0, width)
            dst, src = weave_views(x_bf[g, n][:, PACK * first : PACK * last], picked_view(g, s0 + first, last - first))
            copy(out=dst[:, :, :rows], in_=src[:, :, :rows])
            probe("xw%d%d" % (g, n), x_bf[g, n][:, 0:1])

        def quantise_x(g, n, tag=None):
            s0, width = spans(X_PIECES[g])[n]
            x_words[g, s0] = sbuf([P, width], U32, "x_words%d_%d" % (g, n), tag)
            nc.vector.quantize_mx(
                out=x_words[g, s0][:].bitcast(FP8X4),
                scales=x_scales[g][:, s0 : s0 + width],
                in_=x_bf[g, n][:],
            )
            probe("xq%d%d" % (g, n), x_words[g, s0][:, 0:1])

        w1_bf = {}
        w1_words = [sbuf([P, H], U32, "w1_words%d" % g) for g in range(PASSES)]
        w1_scales = [sbuf([P, H], U8, "w1_scales%d" % g) for g in range(PASSES)]

        def weave_w1(n):
            g, m0, groups = W1_LOADS[n]
            w1_bf[n] = sbuf([P, PACK, groups, PACK], BF16, "w1_bf%d" % n)
            dst = w1_bf[n][:].rearrange("p t m j -> p m j t")
            src = w1_raw[n][:].rearrange("p j (m t) -> p m j t", t=PACK)
            split = W1_ON_VECTOR[n]
            for t0, tiles in spans(W1_TILES[n]):
                ts = slice(t0, t0 + tiles)
                if split > 0:
                    nc.vector.tensor_copy(out=dst[:, :split, :, ts], in_=src[:, :split, :, ts])
                if split < groups:
                    nc.scalar.copy(out=dst[:, split:, :, ts], in_=src[:, split:, :, ts])

        def quantise_w1(n):
            g, m0, groups = W1_LOADS[n]
            for t0, tiles in spans(W1_QUANTISE[n]):
                cols = slice(t0 * P, (t0 + tiles) * P)
                nc.vector.quantize_mx(
                    out=w1_words[g][:, cols].bitcast(FP8X4),
                    scales=w1_scales[g][:, cols],
                    in_=w1_bf[n][:, t0 : t0 + tiles].rearrange("p t m j -> p (t m j)"),
                )
            probe("w1q%d" % n, w1_words[g][:, H - P + m0 : H - P + m0 + 1])

        acc = {}
        banks = 0
        for b, (s0, width) in enumerate(spans(STEPS)):
            sums = BANK // width
            for t0 in range(0, PACK, sums):
                bank = psum.tile([P, sums, width], F32, name="acc%d" % banks, tag="bank%d" % banks)
                banks = banks + 1
                for t in range(t0, t0 + sums):
                    acc[b, t] = (bank, t - t0, sums)

        def first_product_pass(b, g, t, start, stop):
            s0, width = spans(STEPS)[b]
            cols = slice(t * P, (t + 1) * P)
            piece = max(start0 for start0, same in spans(X_PIECES[g]) if start0 <= s0)
            bank, place, sums = acc[b, t]
            nc.tensor.matmul_mx(
                out=bank[:, place, :],
                lhsT=w1_words[g][:, cols].bitcast(FP8X4),
                lhsT_scale=w1_scales[g][:, cols],
                rhs=x_words[g, piece][:, s0 - piece : s0 + width - piece].bitcast(FP8X4),
                rhs_scale=x_scales[g][:, s0 : s0 + width],
                start=start,
                stop=stop,
            )

        def open_pass(g):
            for b in range(OPEN_STEPS):
                tiles = list(range(PACK))
                if g > 0 and b > 0:
                    tiles = list(reversed(tiles))
                for t in tiles:
                    first_product_pass(b, g, t, g == 0 and t == tiles[0], g == PASSES - 1 and t == tiles[-1])

        def closed_step(b):
            for t in reversed(range(PACK)):
                for g in reversed(range(PASSES)):
                    first_product_pass(b, g, t, g == PASSES - 1, g == 0)

        w2_bf = sbuf([P, N * PACK], BF16, "w2_bf")
        w2_scales = sbuf([P, N], U8, "w2_scales")
        h_bf = sbuf([P, S * PACK], BF16, "h_bf")
        h_scales = sbuf([P, S], U8, "h_scales")

        pre = {}

        def add_pos(b):
            s0, width = spans(STEPS)[b]
            pos0 = max(start for start in pos_sb if start <= s0)
            pre[b] = sbuf([P, PACK * width], F32, "pre%d" % b, PRE_BYTES + 2048 * b)
            place = pos_sb[pos0][:, :, s0 - pos0 : s0 - pos0 + width]
            nc.vector.tensor_tensor(
                pre[b][:].rearrange("p (c t i) -> p c t i", t=PACK, i=2),
                acc[b, 0][0][:].rearrange("p t (c i) -> p c t i", i=2),
                place.rearrange("p t (c i) -> p c t i", i=2),
                ADD,
            )

        def hidden(b):
            s0, width = spans(STEPS)[b]
            dst = h_bf[:, PACK * s0 : PACK * (s0 + width)].rearrange("p (c i t) -> p c t i", t=PACK, i=2)
            nc.scalar.activation(dst, pre[b][:].rearrange("p (c t i) -> p c t i", t=PACK, i=2), GELU)
            probe("gelu%d" % b, h_bf[:, PACK * s0 : PACK * s0 + 1])

        def weave_w2(copy):
            dst, src = weave_views(w2_bf[:], w2_raw[:])
            copy(out=dst, in_=src)

        def quantise_w2(tag=None):
            words = sbuf([P, N], U32, "w2_words", tag)
            nc.vector.quantize_mx(out=words[:].bitcast(FP8X4), scales=w2_scales[:], in_=w2_bf[:])
            return words

        res = {}

        def second_product(b, w2_words, tag=None):
            s0, width = spans(OUT_STEPS)[b]
            cols = slice(s0, s0 + width)
            h_words = sbuf([P, width], U32, "h_words%d" % b, tag)
            nc.vector.quantize_mx(
                out=h_words[:].bitcast(FP8X4),
                scales=h_scales[:, cols],
                in_=h_bf[:, PACK * s0 : PACK * (s0 + width)],
            )
            res[b] = psum.tile([P, width], F32, name="res%d" % b, tag="bank%d" % b)
            nc.tensor.matmul_mx(
                out=res[b][:],
                lhsT=w2_words[:].bitcast(FP8X4),
                lhsT_scale=w2_scales[:],
                rhs=h_words[:].bitcast(FP8X4),
                rhs_scale=h_scales[:, cols],
                start=True,
                stop=True,
            )

        staged = {}

        def stage(n, tag=None):
            s0, width = spans(STORES)[n]
            staged[s0] = sbuf([P, width], F32, "staged%d" % n, tag)

        def leave_psum(n, copy):
            s0, width = spans(STORES)[n]
            b = max(b0 for b0, (start0, same) in enumerate(spans(OUT_STEPS)) if start0 <= s0)
            start = spans(OUT_STEPS)[b][0]
            copy(out=staged[s0][:], in_=res[b][:, s0 - start : s0 - start + width])
            probe("copy%d" % n, staged[s0][:, 0:1])

        def store(n):
            s0, width = spans(STORES)[n]
            nc.sync.dma_start(out=out[:, s0 : s0 + width], in_=staged[s0][:])

        for j in range(PACK):
            gather_plane(0, j)
        weave_x(0, 0, nc.vector.tensor_copy)
        weave_x(0, 1, nc.vector.tensor_copy, part=(0, FIRST_PASS_ON_VECTOR))
        weave_x(0, 1, nc.scalar.copy, part=(FIRST_PASS_ON_VECTOR, 512))
        for n in range(len(X_PIECES[0])):
            quantise_x(0, n)
        for j in range(PACK - 1):
            gather_plane(1, j)
        weave_x(1, 0, nc.vector.tensor_copy, rows=PACK - 1, part=(0, P))
        weave_x(1, 0, nc.vector.tensor_copy, rows=PACK - 1, part=(P, 2 * P))
        gather_plane(1, PACK - 1)
        weave_x(1, 1, nc.vector.tensor_copy)
        quantise_x(1, 0)
        quantise_x(1, 1)
        weave_x(1, 2, nc.scalar.copy)
        weave_x(1, 3, nc.scalar.copy)
        weave_w1(0)
        quantise_w1(0)
        open_pass(0)
        quantise_x(1, 2, tag=0)
        weave_w1(1)
        quantise_w1(1)
        open_pass(1)
        quantise_x(1, 3, tag=W1_BYTES)
        weave_w2(nc.scalar.copy)
        w2_words = quantise_w2()
        for b in range(OPEN_STEPS, 5):
            closed_step(b)
        for b in range(EARLY_BEHIND):
            add_pos(b)
            hidden(b)
        second_product(0, w2_words)
        for b in range(5, len(STEPS)):
            closed_step(b)
        stage(0)
        leave_psum(0, nc.scalar.copy)
        store(0)
        for b in range(EARLY_BEHIND, len(STEPS)):
            add_pos(b)
            hidden(b)
        stage(1, POS_BYTES + 16 * 896 + 512)
        stage(2, POS_BYTES + 16 * 896 + 1024)
        stage(3, PRE_BYTES + 2048 * 7)
        stage(4, PRE_BYTES + 2048 * 7 + 1024)
        stage(5)
        second_product(1, w2_words, POS_BYTES + 16 * H_BEHIND)
        for n in range(2, len(OUT_STEPS)):
            second_product(n, w2_words)
        for n in range(1, len(STORES)):
            leave_psum(n, nc.vector.tensor_copy if n in COPIES_ON_VECTOR else nc.scalar.copy)
            store(n)
